import numpy as np, ml_dtypes
CORES = [2,3,42,43,82,83,122,123]
N = 8
import mx_ref
BF = ml_dtypes.bfloat16
def gentries(a):
    return np.ascontiguousarray(a.reshape(8, 16, -1).transpose(0, 2, 1)).reshape(8, -1)
def gtable(e):
    e = np.asarray(e); return np.ascontiguousarray(e.reshape(8, -1, 16).transpose(0, 2, 1)).reshape(128, -1).astype(np.int32)
def gcols(t, e):
    v = np.concatenate([t.reshape(8, 16, -1, 4), np.zeros((8, 16, 1, 4), BF)], axis=2)
    return np.ascontiguousarray(np.stack([v[g][:, e[g]] for g in range(8)])).reshape(128, -1)
def gpick(z, e):
    return np.concatenate([z[16 * g:16 * g + 16][:, e[g]] for g in range(8)])
def tile(rs):
    return np.stack(rs, axis=2).reshape(128, -1).astype(BF)
def pick(q, e):
    c = np.concatenate([q[0].reshape(128, -1, 4), np.zeros((128, 1, 4), np.uint8)], axis=1); s = np.concatenate([q[1], np.ones((16, 1), np.uint8)], axis=1)
    return (np.ascontiguousarray(c[:, e].reshape(128, -1)), np.ascontiguousarray(s[:, e]))
def join(*qs):
    return (np.concatenate([q[0] for q in qs], axis=1), np.concatenate([q[1] for q in qs], axis=1))
def put(q, e, v):
    c, s = q[0].reshape(128, -1, 4).copy(), q[1].copy(); c[:, e] = v[0].reshape(128, -1, 4); s[:, e] = v[1]
    return (c.reshape(128, -1), s)
def pk(c, s):
    return (np.ascontiguousarray(c), mx_ref.live(s))
def emit(q):
    return q[0], q[1]
def packed(v, rng):
    q = [mx_ref.quantize(np.ascontiguousarray(v[r])) for r in range(N)]
    return np.stack([a for a, b in q]), np.stack([mx_ref.plane(b, rng) for a, b in q])
def values_of_codes():
    e, c = np.zeros((128, 128, 4), np.float32), np.zeros((128, 2, 4), np.uint8)
    e[np.arange(128), np.arange(128), 0] = 1
    c[:127, :, 0] = np.arange(256).reshape(2, 128).T[:127]
    return mx_ref.matmul(mx_ref.quantize(e.reshape(128, 512).astype(BF)), (c.reshape(128, 8), np.full((16, 2), 127, np.uint8))).T.reshape(-1).astype(np.float64)
CODE_VALUE, SCALE_VALUE = values_of_codes(), 2.0 ** (np.arange(256) - 127.0)
def decode(q):
    return (CODE_VALUE[q[0]].reshape(16, 8, -1, 4) * SCALE_VALUE[q[1]][:, None, :, None] + 0.0).reshape(128, -1).astype(np.float32)
def f(rng, *shape):
    return mx_ref.flush((rng.standard_normal(shape, dtype=np.float32) * np.exp2(rng.integers(-2, 3, shape[:-1] + (1,)))).astype(BF))
def wide(rng, *shape, cols=0):
    v = rng.standard_normal(shape, dtype=np.float32) * np.exp2(rng.integers(-12, 13, shape)).astype(np.float32)
    if cols: v *= np.repeat(np.exp2(rng.integers(-cols, cols + 1, shape[:-2] + (1, shape[-1] // 4))) * (rng.random(shape[:-2] + (1, shape[-1] // 4)) > 0.0625), 4, axis=-1).astype(np.float32)
    return mx_ref.flush(v.astype(BF))
C = 320
STEP = [1, 2, 4]
GROUP, PLACE = np.arange(8)[:, None], np.arange(C)
def numbers_of(rng):
    return {"x": np.array(f(rng, N, 128, 4 * C)), "u": np.array(f(rng, N, 128, 512)), "v": np.array(f(rng, N, 128, 512))}
def orders(rng):
    return rng.permuted(np.tile(np.arange(C), (N, 8, 1)), axis=2)
def paired(e):
    k = np.zeros_like(e)
    np.put_along_axis(k, e[:, :, 0::2], e[:, :, 1::2], 2)
    np.put_along_axis(k, e[:, :, 1::2], e[:, :, 0::2], 2)
    return k
def stored(p, q, mu):
    return {a: np.stack([gtable(k[r]) for r in range(N)]) for a, k in (("pl", p), ("ql", q), ("ml", mu))}
def lists(rng):
    return stored(paired(orders(rng)), paired(orders(rng)), paired(orders(rng)))
def layers(rng, still=[]):
    w = np.array(f(rng, N, 128, 2048)).reshape(N, 8, 16, 4, 8, 16, 4)
    for i in still:
        w[:, :, i] = 0
        w[:, :, :, :, :, i] = 0
    return w
def weights(rng, w):
    c, s = packed(np.ascontiguousarray(w).reshape(N, 128, 2048), rng)
    return {"wc": c, "ws": s}
def setup_inputs(rng):
    return {**numbers_of(rng), **lists(rng), **weights(rng, layers(rng))}
def setup_inputs_ties(rng):
    d = numbers_of(rng)
    e = orders(rng)
    mu = paired(orders(rng))
    k = np.zeros((N, 8, C))
    for r in range(N):
        h = rng.permutation(8)
        c = rng.integers(0, C, 2)
        k[r, h[1], min(c[0], mu[r, h[1], c[0]])] = -1
        k[r, h[2], max(c[1], mu[r, h[2], c[1]])] = -1
        k[r, h[3], e[r, h[3], :2]] = -1
        k[r, h[4]] = rng.integers(-4, 0, C)
        k[r, h[5]] = rng.integers(-1, 3, C)
        k[r, h[6]] = rng.integers(1, 4, C)
        k[r, h[7]] = rng.integers(0, 2, C)
        k[r, h[7], e[r, h[7], 0]] = -1
        k[r, h[7], e[r, h[7], 2 * rng.integers(1, C // 2)]] = -1
    x = d["x"].reshape(N, 8, 16, C, 4)
    x[:, :, 0] = 0
    x[:, :, 0, :, 0] = k.astype(np.float32).astype(BF)
    u = d["u"].reshape(N, 128, 128, 4)
    u[:, :, ::16] = 0
    for h in range(0, 128, 16): u[:, h, h, 0] = 1
    return {"x": x.reshape(N, 128, 4 * C), "u": u.reshape(N, 128, 512), "v": d["v"], **stored(paired(e), paired(np.roll(e, -1, axis=2)), mu), **weights(rng, layers(rng, [0]))}
def setup_inputs_near(rng):
    d = numbers_of(rng)
    x = d["x"].astype(np.float32).reshape(N, 8, 16, C, 4)
    x[:, :, :2] = 0
    x[:, :, 8:] = 0
    x[:, :, 1, :, 0] = rng.choice([-1.0, 1.0], (N, 8, C)) * (1.0 + 0.125 * rng.integers(0, 8, (N, 8, C))) * 2.0 ** -7
    u = d["u"].reshape(N, 128, 128, 4)
    u[:, :, ::16] = 0
    w = layers(rng, [0, 1, 8, 9, 10, 11, 12, 13, 14, 15])
    o = rng.permutation(N) % 4
    for r in range(N):
        c = rng.choice([-1.0, 1.0], (8, 1))
        s = rng.integers(0, 16, (8, C))
        digits = ((s[:, :, None] >> np.arange(4)) & 1) * np.exp2(np.arange(4) - 23.0)
        if o[r] < 2:
            x[r, :, 0, :, 0] = c
            x[r, :, 8] = digits
            x[r, :, 11, :, 0] = 2.0 ** -10
        elif o[r] == 2: x[r, :, 8] = digits * rng.choice([-1.0, 1.0], (8, C, 1))
        else:
            x[r, :, 8, :, 0] = np.where(s < 8, 1.25, 0.0) * 2.0 ** -29 * c
            x[r, :, 9, :, 0] = np.where(s < 8, 0.0, 1.125) * 2.0 ** -29 * c
            x[r, :, 12, :, 0] = 2.0 ** -28
            for g in range(8): w[r, g, 1, 0, g, 10, 0] = 2.0 ** -30
            for i, g in enumerate(rng.permutation(8)[:4]):
                if i < 2:
                    e = rng.choice([-1.0, 1.0], C) * 2.0 ** -29
                    x[r, g, 8, :, 0] = 1.25 * e
                    x[r, g, 9, :, 0] = -1.125 * e
                else:
                    x[r, g, 8:] = 0
                    x[r, g, 12, :, 0] = 2.0 ** -30
                    w[r, g, 1, 0, g, 10, 0] = -2.0 ** -30
                    w[r, g, 1, 0, g, 11, 0] = 2.0 ** -30
        at = [0, C - 1, int(rng.integers(C)), int(rng.integers(C))]
        for g, j in zip(rng.permutation(8)[:4], at): x[r, g, 0, j, 0] = 2.0 ** 29 * rng.choice([-1.0, 1.0])
        k = 1.0 if o[r] == 0 else 2.0 ** -30
        for h in range(0, 128, 16):
            u[r, h, h, 0] = k if o[r] < 2 else 1.0
            if o[r] < 2: u[r, h + 11, h, 0] = k
            if o[r] < 3: u[r, h + 8, h] = k
            else:
                u[r, h + 8, h, 0] = k
                u[r, h + 9, h, 0] = 1.125 * k
                u[r, h + 10, h, 0] = k
                u[r, h + 11, h, 0] = 1.125 * k
    return {"x": x.reshape(N, 128, 4 * C).astype(BF), "u": u.reshape(N, 128, 512), "v": d["v"], **lists(rng), **weights(rng, w)}
def setup_inputs_odd(rng):
    d = numbers_of(rng)
    x = (1.0 + (2 * rng.integers(0, 64, (N, 16, 8, C, 4)) + 1) * 2.0 ** -7) * np.exp2(-rng.integers(0, 7, (N, 16, 8, C, 4)).astype(np.float64)) * rng.choice([-1.0, 1.0], (N, 16, 8, C, 4))
    x[:, :, 0, :, 0] = 1.96875 * 2.0 ** 8 * rng.choice([-1.0, 1.0], (N, 16, C))
    x[:, 1::2, 0, :, 0] *= np.where(rng.random((N, 8, C)) < 0.5, 2.0 ** -6, 1.0)
    u = d["u"].reshape(N, 16, 8, 128, 4)
    u[:, :, 0, ::16] = 0
    for r in range(N):
        for i, g in enumerate(rng.permutation(8)[:4]):
            x[r, 2 * g, 1, :, 0] = (8 + rng.integers(0, 2, C)) * 2.0 ** (i - 8)
            u[r, :, :, 16 * g] = 0
            u[r, 2 * g, 1, 16 * g, 0] = 1.0
    return {"x": x.astype(np.float32).reshape(N, 128, 4 * C).astype(BF), "u": u.reshape(N, 128, 512), "v": d["v"], **lists(rng), **weights(rng, layers(rng, [0, 8]))}
def setup_inputs_ends(rng):
    d = numbers_of(rng)
    o, e = rng.permutation(N) % 2, rng.permutation(N) % 4
    sign = rng.choice([-1.0, 1.0], (128, 1, 4))
    half = np.repeat(rng.choice([0.5, 1.0], (N, 1, C, 2)), 2, axis=3)
    small = sign * (1.0 + 0.125 * rng.integers(0, 8, (N, 128, C, 4))) * 2.0 ** -30
    x = sign * half * (14 + rng.integers(0, 3, (N, 128, C, 4))) * 2.0 ** 26
    x[o == 1] = small[o == 1]
    x[:, 112:120] = sign[112:120]
    x[:, 120:] = small[:, 120:]
    size = np.where(o == 0, 2.0 ** 30, 2.0 ** -30)
    kinds = np.array([[1, 1, 1, 1]] * 2 + [[-1, -1, -1, -1]] * 3 + [[1, 1, -1, -1]] * 2 + [[0, 0, 0, 0]])
    u = d["u"].astype(np.float32).reshape(N, 128, 128, 4)
    for r in range(N): u[r, :, ::16] = sign * kinds[rng.permutation(8)][None] * size[r]
    u[:, 112:, ::16] = 0
    v = rng.choice([-1.0, 1.0], (N, 128, 512)) * size[:, None, None]
    a = orders(rng)
    p, q, mu = paired(a), paired(np.roll(a, -1, axis=2)), paired(orders(rng))
    q[e == 1] = p[e == 1]
    mu[e == 1] = p[e == 1]
    p[e == 2] = C - 1 - np.arange(C)
    q[e == 2] = np.arange(C) ^ 1
    q[e == 3] = paired(orders(rng))[e == 3]
    w = np.zeros((N, 128, 4, 128, 4), np.float32)
    i, n = np.arange(112), np.arange(8)
    for b in range(4):
        for r in range(N):
            if o[r] == 0: w[r, i, b, i, b] = -4.0
            w[r, (120 if b < 2 else 96) + n, b, 112 + n, b] = 2.0 ** 30 if b < 2 else 2.0 ** -30
    return {"x": x.astype(np.float32).reshape(N, 128, 4 * C).astype(BF), "u": u.reshape(N, 128, 512).astype(BF), "v": v.astype(np.float32).astype(BF), **stored(p, q, mu), **weights(rng, w.astype(BF))}
def setup_inputs_spread(rng):
    d = setup_inputs(rng)
    d["x"] = wide(rng, N, 128, 4 * C, cols=6)
    return d
def check_inputs(d):
    b = []
    for k in ("x", "u", "v"):
        a = np.abs(d[k].astype(np.float32))
        if not (np.isfinite(a).all() and ((a == 0) | (a >= 2.0 ** -30) & (a <= 2.0 ** 30)).all()): b.append("a value of " + k)
    for k in ("pl", "ql", "ml"):
        for r in range(N):
            e = gentries(d[k][r])
            if not ((e >= 0) & (e < C)).all(): b.append("an entry of " + k)
            elif (e == PLACE).any() or (e[GROUP, e] != PLACE).any(): b.append(k + ": no involution without fixed points")
    none, least, most = [emit(mx_ref.quantize(np.full((128, 16), k, np.float32).astype(BF)))[1][0, 0] for k in (0.0, 2.0 ** -30, 2.0 ** 30)]
    for r in range(N):
        if ((d["wc"][r] == 0x7F) | (d["wc"][r] == 0xFF)).any(): b.append("wc: a code that is no number")
        s = mx_ref.live(d["ws"][r])
        if ((s != none) & ((s < least) | (s > most))).any(): b.append("ws: a scale out of range")
        if (((d["wc"][r].reshape(16, 8, 512, 4) & 0x7F) != 0) & (s == none)[:, None, :, None]).any(): b.append("wc: a code other than zero under the scale of zeros")
    return b
def powers(a):
    k = [np.tile(PLACE, (8, 1))]
    for i in range(C // 2 - 1): k.append(a[GROUP, k[-1]])
    return np.stack(k)
def mirror(p, q, stop):
    ahead, back = powers(q[GROUP, p]), powers(p[GROUP, q])
    i, j = np.argmax(stop[GROUP, ahead], axis=0), np.argmax(stop[GROUP, back], axis=0)
    return ahead[i, GROUP, back[j, GROUP, PLACE]]
def reference(x, u, v, pl, ql, ml, wc, ws):
    qu = [mx_ref.quantize(u[r]) for r in range(N)]
    lay = [pk(wc[r], ws[r]) for r in range(N)]
    p, q, mu = [[gentries(a[r]).astype(np.int64) for r in range(N)] for a in (pl, ql, ml)]
    now = [x[r] for r in range(N)]
    for step in STEP:
        own, sent, image = [], [], []
        for r in range(N):
            t = mx_ref.quantize(now[r])
            s = mx_ref.matmul(qu[r], t)[::16] + np.float32(0.0)
            d = decode(t).astype(BF)
            m = mirror(p[r], q[r], s < 0)
            z = (gcols(d, m).astype(np.float32) + gcols(d, q[r][GROUP, p[r]]).astype(np.float32)) * np.float32(0.5)
            sent.append(mx_ref.quantize(z.astype(BF)))
            w = (PLACE < mu[r]) & (s[GROUP, m] > s[GROUP, m[GROUP, mu[r]]])
            e = np.where(w | w[GROUP, mu[r]], mu[r], PLACE)
            q[r] = e[GROUP, q[r][GROUP, e]]
            own.append(d)
            image.append(m)
        now = [tile([gpick(mx_ref.matmul(pick(lay[r], np.arange(128 * b, 128 * b + 128)), sent[r ^ step]) * np.float32(0.03125), image[r]) + own[r][:, b::4].astype(np.float32) for b in range(4)]) for r in range(N)]
    y, qo = np.zeros((N, 128, C), np.float32), np.zeros((N, 8, C), np.float32)
    oc, osc = np.zeros((N, 128, 4 * C), np.uint8), np.zeros((N, 16, C), np.uint8)
    for r in range(N):
        t = mx_ref.quantize(now[r])
        y[r] = mx_ref.matmul(mx_ref.quantize(v[r]), t)
        qo[r] = q[r]
        oc[r], osc[r] = emit(t)
    return {"y": y, "qo": qo, "oc": oc, "osc": osc}

@@ -1,0 +1,398 @@
+from concourse.bass import DstId, RemoteDMATransfer
+from concourse.mybir import dt, AluOpType as OP, ActivationFunctionType as AF
+
+C = 320
+K = C // 16
+STEP = [1, 2, 4]
+STAGES = [3, 3, 3, 3, 2]
+BIG = 1024.0
+SLOPE, SHIFT = 164, -51997
+UNMET = 162
+NCELL = 53000
+
+SCRATCH = {
+    "x0": ("sbuf", [128, 4 * C], "bfloat16"), "xn": ("sbuf", [128, 4 * C], "bfloat16"), "zt": ("sbuf", [128, 4 * C], "bfloat16"), "ut": ("sbuf", [128, 512], "bfloat16"), "vt": ("sbuf", [128, 512], "bfloat16"),
+    "uc": ("sbuf", [128, 128], "float8_e4m3fn_x4"), "us": ("sbuf", [128, 128], "uint8"),
+    "urc": ("sbuf", [128, 128], "float8_e4m3fn_x4"), "urs": ("sbuf", [128, 128], "uint8"),
+    "vc": ("sbuf", [128, 128], "float8_e4m3fn_x4"), "vs": ("sbuf", [128, 128], "uint8"),
+    "lc": ("sbuf", [128, 512], "float8_e4m3fn_x4"), "ls": ("sbuf", [128, 512], "uint8"),
+    "ec": ("sbuf", [128, 512], "float8_e4m3fn_x4"), "es": ("sbuf", [128, 512], "uint8"),
+    "eone": ("sbuf", [128, 516], "bfloat16"), "ebase": ("sbuf", [128, 516], "bfloat16"),
+    "qpi": ("sbuf", [128, C], "int32"), "mpi": ("sbuf", [128, C], "int32"),
+    "pli": ("sbuf", [128, K], "int32"), "mli": ("sbuf", [128, K], "int32"),
+    "pu": ("sbuf", [128, K], "uint16"), "mu16": ("sbuf", [128, K], "uint16"),
+    "lowu": ("sbuf", [128, K], "uint16"), "highu": ("sbuf", [128, K], "uint16"),
+    "muf": ("sbuf", [128, K], "float32"), "tlo": ("sbuf", [128, K], "float32"), "thi": ("sbuf", [128, K], "float32"),
+    "ji": ("sbuf", [128, C], "int32"), "ja": ("sbuf", [128, C], "int32"), "jf": ("sbuf", [128, C], "float32"),
+    "md": ("sbuf", [128, C], "float32"),
+    "pi1": ("sbuf", [128, 1], "int32"), "pa1": ("sbuf", [128, 1], "int32"), "pf1": ("sbuf", [128, 1], "float32"),
+    "p20": ("sbuf", [128, 1], "float32"), "qoff": ("sbuf", [128, 1], "float32"),
+    "k16": ("sbuf", [128, K], "int32"), "k1": ("sbuf", [128, K], "int32"), "u8i": ("sbuf", [128, 8], "int32"),
+    "coff": ("sbuf", [128, K], "float32"), "c640": ("sbuf", [128, K], "float32"),
+    "piu": ("sbuf", [128, K], "uint16"), "upick": ("sbuf", [128, 8], "uint16"),
+    "cb": ("sbuf", [128, C], "bfloat16"),
+    "wa": ("sbuf", [128, 2 * C], "float32"), "wb": ("sbuf", [128, 2 * C], "float32"),
+    "d0": ("sbuf", [128, 2 * C], "float32"), "d1": ("sbuf", [128, 2 * C], "float32"), "d2": ("sbuf", [128, 2 * C], "float32"), "d3": ("sbuf", [128, 2 * C], "float32"),
+    "lw": ("sbuf", [128, 3 * C], "float32"), "lg": ("sbuf", [128, C], "float32"),
+    "tab": ("sbuf", [128, NCELL], "bfloat16"),
+    "qq": ("sbuf", [128, 2 * C], "float32"), "qr": ("sbuf", [128, 2 * C], "float32"), "cm": ("sbuf", [128, 2 * C], "float32"),
+    "aw": ("sbuf", [128, C], "float32"), "f320": ("sbuf", [128, C], "float32"), "ssb": ("sbuf", [128, C], "float32"),
+    "sc0": ("sbuf", [128, C], "float32"), "sc1": ("sbuf", [128, C], "float32"), "sc2": ("sbuf", [128, C], "float32"),
+    "nf": ("sbuf", [128, K], "float32"), "nfk": ("sbuf", [128, K], "float32"),
+    "wf": ("sbuf", [128, K], "float32"), "wg": ("sbuf", [128, K], "float32"), "gg": ("sbuf", [128, K], "float32"),
+    "df": ("sbuf", [128, K], "float32"), "t1": ("sbuf", [128, K], "float32"), "t2": ("sbuf", [128, K], "float32"),
+    "t3": ("sbuf", [128, K], "float32"), "t4": ("sbuf", [128, K], "float32"), "t5": ("sbuf", [128, K], "float32"),
+    "t6": ("sbuf", [128, K], "float32"), "t7": ("sbuf", [128, K], "float32"),
+    "wu": ("sbuf", [128, K], "uint16"), "wz": ("sbuf", [128, K], "uint16"), "lu": ("sbuf", [128, K], "uint16"),
+    "k1u": ("sbuf", [128, K], "uint16"), "k2u": ("sbuf", [128, K], "uint16"),
+    "sgu": ("sbuf", [128, K], "uint16"), "qsu": ("sbuf", [128, K], "uint16"),
+    "mw": ("sbuf", [128, C], "float32"), "sm": ("sbuf", [128, C], "float32"), "smh": ("sbuf", [128, C], "float32"),
+    "sw": ("sbuf", [128, C], "float32"), "sgw": ("sbuf", [128, C], "float32"), "qs": ("sbuf", [128, C], "float32"),
+    "fo": ("sbuf", [128, 4 * C], "bfloat16"), "fh": ("sbuf", [128, 4 * C], "bfloat16"), "fa": ("sbuf", [128, 4 * C], "bfloat16"),
+    "rs": ("sbuf", [128, 4 * C], "float32"), "yo": ("sbuf", [128, C], "float32"),
+    "pa": ("psum", [128, 2048], "float32"), "pb": ("psum", [128, 2048], "float32"),
+}
+for _r in range(3):
+    SCRATCH["zc%d" % _r] = ("sbuf", [128, C], "float8_e4m3fn_x4")
+    SCRATCH["zs%d" % _r] = ("sbuf", [128, C], "uint8")
+    SCRATCH["ac%d" % _r] = ("sbuf", [128, C], "float8_e4m3fn_x4")
+    SCRATCH["as%d" % _r] = ("sbuf", [128, C], "uint8")
+    SCRATCH["am%d" % _r] = ("sbuf", [128, K], "uint16")
+    SCRATCH["aa%d" % _r] = ("sbuf", [128, K], "uint16")
+    SCRATCH["mo%d" % _r] = ("sbuf", [128, K], "uint16")
+    SCRATCH["ao%d" % _r] = ("sbuf", [128, K], "uint16")
+for _r in range(4):
+    SCRATCH["tc%d" % _r] = ("sbuf", [128, C], "float8_e4m3fn_x4")
+    SCRATCH["ts%d" % _r] = ("sbuf", [128, C], "uint8")
+
+SEMAPHORES = ["qV", "qS", "qT", "qG", "sent", "stored"] + ["ld_" + n for n in ("x", "u", "v", "wc", "ws", "pl", "ml", "qw", "mw")]
+for _r in range(3):
+    SEMAPHORES += ["arX%d" % _r, "arA%d" % _r, "arM%d" % _r]
+
+
+def make_queues(g, T):
+    queues = {"V": g.vector, "S": g.scalar, "T": g.tensor, "G": g, "Y": g.sync}
+    count = {"V": 0, "S": 0, "T": 0, "G": 0}
+    clocks = {}
+    known = {q: {} for q in queues}
+    writer, readers = {}, {}
+
+    def merge(a, b):
+        for k, n in b.items():
+            if a.get(k, 0) < n:
+                a[k] = n
+
+    def need(q, sem, n):
+        if known[q].get(sem, 0) >= n:
+            return
+        queues[q].wait_ge(T.sem[sem], n)
+        if (sem, n) in clocks:
+            merge(known[q], clocks[(sem, n)])
+        known[q][sem] = n
+
+    def waits(q, reads, writes):
+        own = "q" + q
+        want = {}
+        for k in reads:
+            if k in writer:
+                s, n = writer[k]
+                want[s] = max(want.get(s, 0), n)
+        for k in writes:
+            if k in writer:
+                s, n = writer[k]
+                want[s] = max(want.get(s, 0), n)
+            for s, n in readers.get(k, {}).items():
+                if s != own:
+                    want[s] = max(want.get(s, 0), n)
+        for s, n in want.items():
+            need(q, s, n)
+
+    def note(sem, n, reads, writes):
+        for k in reads:
+            r = readers.setdefault(k, {})
+            r[sem] = max(r.get(sem, 0), n)
+        for k in writes:
+            writer[k] = (sem, n)
+            readers[k] = {}
+
+    def op(q, fn, reads, writes):
+        waits(q, reads, writes)
+        inst = fn(queues[q])
+        count[q] += 1
+        sem = "q" + q
+        inst.then_inc(T.sem[sem], 1)
+        c = dict(known[q])
+        merge(c, clocks.get((sem, count[q] - 1), {}))
+        c[sem] = count[q]
+        clocks[(sem, count[q])] = c
+        note(sem, count[q], reads, writes)
+
+    def dma(q, pairs, sem, total, reads, writes):
+        waits(q, reads, writes)
+        for out, in_ in pairs:
+            queues[q].dma_start(out, in_).then_inc(T.sem[sem], 16)
+        note(sem, total, reads, writes)
+
+    def arrives(sem, total, writes):
+        note(sem, total, [], writes)
+
+    return op, dma, arrives, waits, need, count
+
+
+def rank_program(g, core, T, topo):
+    rank = T.rank_of(core)
+    if rank is None:
+        return
+    op, dma, arrives, waits, need, count = make_queues(g, T)
+    sent = [0]
+
+    def A(name, a=0, b=None):
+        return T[name][:, a:b] if b is not None else T[name][:]
+
+    def send(dst, out, in_, sem, key):
+        waits("G", [key], [])
+        rid, pid, _ = topo.addr(dst)
+        m = topo.mask(core, dst)
+        g.remote_dma(out, in_, T.sem[sem], T.sem.sent, pid, rid, m)
+        sent[0] += len(topo.engines(core, dst))
+
+    def copy(q, out, in_, reads, writes, scale=None):
+        if q == "S":
+            if scale is None:
+                op("S", lambda e: e.activation(out, in_, AF.Copy), reads, writes)
+            else:
+                op("S", lambda e: e.activation(out, in_, AF.Copy, 0.0, scale), reads, writes)
+        else:
+            op("V", lambda e: e.tensor_copy(out, in_), reads, writes)
+
+    def tt(out, a, b, o, reads, writes):
+        op("V", lambda e: e.tensor_tensor(out, a, b, o), reads, writes)
+
+    def ts(out, a, s1, o1, reads, writes, s2=None, o2=None):
+        if o2 is None:
+            op("V", lambda e: e.tensor_scalar(out, a, s1, None, o1), reads, writes)
+        else:
+            op("V", lambda e: e.tensor_scalar(out, a, s1, s2, o1, o2), reads, writes)
+
+    def ind(win, off, a=0, b=C):
+        return T[win][:, a:b].indirect(T[off][:, 0:K])
+
+    def scan(dst, src, key):
+        op("V", lambda e: e.tensor_tensor_scan(T[dst][:], T.md[:], T[src][:, 0:C], 0.0, OP.add, OP.max), ["md", key], [dst])
+
+    def ends(sc):
+        return T[sc][:, 15:C:16]
+
+    def take(out, sc, extra=None, o=None):
+        ts(T[out][:], ends(sc), T.qoff[:, 0:1], OP.subtract, [sc, "qoff"], [out], extra, o)
+
+    def mm(bank, n, lc, ls, rc, rs, reads, a):
+        buf, b = bank
+        op("T", lambda e: e.matmul_mx(T[buf][:, 512 * b:512 * b + n], T[lc][:, a:a + 128], T[ls][:, a:a + 128], T[rc][:], T[rs][:], True, True), reads, [(buf, b)])
+
+    dma("S", [(T.x0[:], T.x[:])], "ld_x", 16, [], ["x0"])
+    dma("S", [(T.ut[:], T.u[:])], "ld_u", 16, [], ["ut"])
+    dma("Y", [(T.pli[:], T.pl[:])], "ld_pl", 16, [], ["pli"])
+    dma("Y", [(T.qpi[i:128:16, :], T.ql[:]) for i in range(16)], "ld_qw", 256, [], ["qpi"])
+    dma("S", [(T.lc[:].bitcast(dt.uint8), T.wc[:])], "ld_wc", 16, [], ["lc"])
+    dma("S", [(T.ls[:], T.ws[:])], "ld_ws", 16, [], ["ls"])
+    dma("Y", [(T.mli[:], T.ml[:])], "ld_ml", 16, [], ["mli"])
+    dma("Y", [(T.mpi[i:128:16, :], T.ml[:]) for i in range(16)], "ld_mw", 256, [], ["mpi"])
+    dma("Y", [(T.vt[:], T.v[:])], "ld_v", 16, [], ["vt"])
+    for r in range(3):
+        e = len(topo.engines(T.cores[rank ^ STEP[r]], core))
+        arrives("arX%d" % r, 2 * e, ["ac%d" % r, "as%d" % r])
+        arrives("arA%d" % r, e, ["aa%d" % r])
+        arrives("arM%d" % r, e, ["am%d" % r])
+
+    def iota(name, a, b, step, base, mult, flag=False):
+        op("G", lambda e: e.iota(T[name][:, a:b], [[step, b - a]], base, mult, allow_small_or_imprecise_dtypes=True) if flag else e.iota(T[name][:, a:b], [[step, b - a]], base, mult), [], [name])
+    iota("pi1", 0, 1, 1, 0, 1)
+    iota("ji", 0, C, 1, 4096, -1)
+    iota("k1", 0, K, 1, 0, 0)
+    iota("k16", 0, K, 16, 0, 0)
+    iota("u8i", 0, 8, 16, 0, 0)
+    op("V", lambda e: e.memset(T.eone[:], 1.0), [], ["eone"])
+    op("G", lambda e: e.affine_select(T.ebase[:], T.eone[:], [[-1, 516]], OP.is_equal, 0.0, 3, 4), ["eone"], ["ebase"])
+    iota("wa", C, 2 * C, 1, C, 0, True)
+    iota("wb", C, 2 * C, 1, C, 0, True)
+    iota("cb", 0, C, 1, -160, 0, True)
+    iota("cm", 0, C, 1, 0, 0, True)
+    ts(T.pa1[:], T.pi1[:], 15, OP.bitwise_and, ["pi1"], ["pa1"])
+    ts(T.pf1[:], T.pa1[:], 1.0, OP.mult, ["pa1"], ["pf1"])
+    ts(T.ja[:], T.ji[:], 15, OP.bitwise_and, ["ji"], ["ja"])
+    ts(T.p20[:], T.pf1[:], 20.0, OP.mult, ["pf1"], ["p20"])
+    ts(T.qoff[:], T.pf1[:], -BIG, OP.mult, ["pf1"], ["qoff"], 15 * BIG, OP.add)
+    ts(T.jf[:], T.ja[:], 0.0, OP.is_equal, ["ja"], ["jf"], -33 * BIG, OP.mult)
+    ts(T.piu[:], T.k1[:], T.p20[:, 0:1], OP.add, ["k1", "p20"], ["piu"])
+    ts(T.coff[:], T.k16[:], T.pf1[:, 0:1], OP.add, ["k16", "pf1"], ["coff"])
+    ts(T.md[:], T.jf[:], BIG, OP.add, ["jf"], ["md"])
+    ts(T.c640[:], T.coff[:], float(2 * C), OP.add, ["coff"], ["c640"])
+    copy("V", T.upick[:], T.u8i[:], ["u8i"], ["upick"])
+    op("V", lambda e: e.memset(T.d0[:, 0:C], 1.0), [], ["d0"])
+    op("V", lambda e: e.memset(T.d0[:, C:2 * C], 0.0), [], ["d0"])
+    for n in ("d1", "d2", "d3"):
+        op("V", (lambda n: lambda e: e.memset(T[n][:, C:2 * C], 0.0))(n), [], [n])
+    op("V", lambda e: e.memset(T.lw[:], float(2 * UNMET)), [], ["lw"])
+
+    def quant(c, s, t, a=0, b=None, ca=0, cb=None):
+        cv = T[c][:, ca:cb] if cb else T[c][:]
+        sv = T[s][:, ca:cb] if cb else T[s][:]
+        tv = T[t][:, a:b] if b else T[t][:]
+        op("V", lambda e: e.quantize_mx(cv, sv, tv), [t], [c, s])
+
+    for b in range(4):
+        quant("ec", "es", "ebase", 3 - b, 3 - b + 512, 128 * b, 128 * b + 128)
+    copy("V", T.pu[:], T.pli[:], ["pli"], ["pu"])
+    copy("V", T.qq[:, 0:C], ind("qpi", "piu"), ["qpi", "piu"], ["qq"])
+    copy("V", T.aw[:], ind("qq", "pu"), ["qq", "pu"], ["aw"])
+    scan("sc0", "aw", "aw")
+    take("ao0", "sc0")
+    quant("uc", "us", "ut")
+    op("V", lambda e: e.tensor_copy(T.urc[:].bitcast(dt.uint32), T.uc[:].bitcast(dt.uint32).indirect(T.upick[:, 0:8])), ["uc", "upick"], ["urc"])
+    op("S", lambda e: e.activation(T.urs[:], T.us[:].indirect(T.upick[:, 0:8]), AF.Copy), ["us", "upick"], ["urs"])
+    quant("tc0", "ts0", "x0")
+
+    qcur, qnew = "qq", "qr"
+    for r in range(3):
+        partner = T.cores[rank ^ STEP[r]]
+        tc, tsn = "tc%d" % r, "ts%d" % r
+        ao, mo, aa, am, ac, asn = "ao%d" % r, "mo%d" % r, "aa%d" % r, "am%d" % r, "ac%d" % r, "as%d" % r
+        send(partner, T[ac][:].bitcast(dt.uint8), T[tc][:].bitcast(dt.uint8), "arX%d" % r, tc)
+        send(partner, T[asn][:], T[tsn][:], "arX%d" % r, tsn)
+        send(partner, T[aa][:], T[ao][:], "arA%d" % r, ao)
+        mm(("pb", 0), C, "urc", "urs", tc, tsn, ["urc", "urs", tc, tsn], 0)
+        for b in range(4):
+            mm(("pa", b), C, "ec", "es", tc, tsn, ["ec", "es", tc, tsn], 128 * b)
+        ts(T.f320[:], T.pb[:, 0:C], 0.0, OP.is_lt, [], ["f320", ("pb", 0)], float(C), OP.mult)
+        tt(T.wa[:, 0:C], ind("f320", ao), T.aw[:], OP.add, ["f320", ao, "aw"], ["wa"])
+        copy("S", T.ssb[:], T.pb[:, 0:C], [], ["ssb", ("pb", 0)])
+        for b in range(4):
+            mm(("pb", b), C, "ec", "es", ac, asn, ["ec", "es", ac, asn], 128 * b)
+        scan("sc0", "wa", "wa")
+        take("wu", "sc0")
+
+        def half(b):
+            copy("S", T.fh[:, C * b:C * b + C], T.pb[:, 512 * b:512 * b + C], [], [("fh", b), ("pb", b)], 0.5)
+
+        def ahead(b):
+            copy("S", T.fa[:, C * b:C * b + C], ind("fh", aa, C * b, C * b + C), [("fh", b), aa], [("fa", b)])
+
+        lists = ["wu", "wz"]
+        src, oth = "wa", "wb"
+        dcur, free = "d0", ["d1", "d2", "d3"]
+        for i, k in enumerate(STAGES):
+            lst = lists[i % 2]
+            wsrc, dsrc = src, dcur
+            used = []
+            for j in range(k - 1):
+                dst = oth if wsrc == src else src
+                copy("S", T[dst][:, 0:C], ind(wsrc, lst, 0, 2 * C), [wsrc, lst], [dst])
+                dn = [n for n in free if n != dsrc and n != dcur and n not in used][0]
+                if i == 0:
+                    ts(T[dn][:, 0:C], ind(dsrc, lst, 0, 2 * C), 1.0, OP.add, [dsrc, lst], [dn])
+                else:
+                    tt(T[dn][:, 0:C], ind(dsrc, lst, 0, 2 * C), T.smh[:], OP.add, [dsrc, lst, "smh"], [dn])
+                used.append(dn)
+                wsrc, dsrc = dst, dn
+            if wsrc != src:
+                src, oth = oth, src
+            dcur = dsrc
+            if i < len(STAGES) - 1:
+                copy("S", T.smh[:], T[dcur][:, 0:C], [dcur], ["smh"])
+            if i < len(STAGES) - 1:
+                scan("sc0", src, src)
+                take(lists[(i + 1) % 2], "sc0")
+            if i == 0:
+                scan("sc1", "f320", "f320")
+                ts(T.nf[:], ends("sc1"), T.qoff[:, 0:1], OP.subtract, ["sc1", "qoff"], ["nf"], 0.0, OP.is_equal)
+                tt(T.nfk[:], T.nf[:], T.c640[:], OP.mult, ["nf", "c640"], ["nfk"])
+            if r == 0 and i == 1:
+                copy("V", T.mu16[:], T.mli[:], ["mli"], ["mu16"])
+                copy("V", T.muf[:], T.mli[:], ["mli"], ["muf"])
+                tt(T.tlo[:], T.muf[:], T.coff[:], OP.min, ["muf", "coff"], ["tlo"])
+                tt(T.thi[:], T.muf[:], T.coff[:], OP.max, ["muf", "coff"], ["thi"])
+                copy("V", T.lowu[:], T.tlo[:], ["tlo"], ["lowu"])
+                copy("V", T.highu[:], T.thi[:], ["thi"], ["highu"])
+            if i >= 2:
+                half(i - 2)
+        half(3)
+        scan("sc0", src, src)
+        take("wf", "sc0")
+        take("wu", "sc0")
+        tt(T.t1[:], T.wf[:], T.nfk[:], OP.max, ["wf", "nfk"], ["t1"])
+        copy("V", T.lu[:], T.t1[:], ["t1"], ["lu"])
+        op("V", (lambda d: lambda e: e.tensor_copy(T.lw[:].indirect(T.lu[:, 0:K]), T[d][:, 0:C]))(dcur), ["lu", dcur], ["lw"])
+        copy("S", T.lg[:], ind("lw", "wu", 0, 2 * C), ["lw", "wu"], ["lg"])
+        scan("sc1", dcur, dcur)
+        ts(T.wg[:], T.wf[:], float(SLOPE), OP.mult, ["wf"], ["wg"], float(SHIFT), OP.add)
+        take("df", "sc1")
+        tt(T.gg[:], T.wf[:], T.wg[:], OP.max, ["wf", "wg"], ["gg"])
+        tt(T.t2[:], T.df[:], T.nf[:], OP.mult, ["df", "nf"], ["t2"])
+        tt(T.t3[:], T.gg[:], T.t2[:], OP.add, ["gg", "t2"], ["t3"])
+        tt(T.t4[:], T.gg[:], T.df[:], OP.subtract, ["gg", "df"], ["t4"])
+        copy("V", T.k1u[:], T.t3[:], ["t3"], ["k1u"])
+        ts(T.t5[:], T.t4[:], T.qoff[:, 0:1], OP.subtract, ["t4", "qoff"], ["t5"])
+        op("V", lambda e: e.tensor_copy(T.tab[:].indirect(T.k1u[:, 0:K]), T.cb[:]), ["k1u", "cb"], ["tab"])
+        scan("sc2", "lg", "lg")
+        tt(T.t6[:], ends("sc2"), T.t5[:], OP.add, ["sc2", "t5"], ["t6"])
+        copy("V", T.k2u[:], T.t6[:], ["t6"], ["k2u"])
+        ts(T.mw[:], T.tab[:].indirect(T.k2u[:, 0:K]), 160.0, OP.add, ["tab", "k2u"], ["mw"])
+        ahead(0)
+        ahead(1)
+        scan("sc0", "mw", "mw")
+        take(mo, "sc0")
+        send(partner, T[am][:], T[mo][:], "arM%d" % r, mo)
+        if r == 0:
+            copy("V", T.cm[:, C:2 * C], ind("mpi", "piu"), ["mpi", "piu"], ["cm"])
+            copy("V", T.qq[:, C:2 * C], ind("qq", "mu16"), ["qq", "mu16"], [("qq", 1)])
+        copy("V", T.sm[:], ind("ssb", mo), ["ssb", mo], ["sm"])
+        ahead(2)
+        copy("S", T.smh[:], ind("sm", "highu"), ["sm", "highu"], ["smh"])
+        tt(T.sw[:], ind("sm", "lowu"), T.smh[:], OP.is_gt, ["sm", "lowu", "smh"], ["sw"])
+        ahead(3)
+        scan("sc1", "sw", "sw")
+        take("t7", "sc1", float(C), OP.mult)
+        tt(T.t7[:], T.t7[:], T.coff[:], OP.add, ["t7", "coff"], ["t7"])
+        copy("V", T.sgu[:], T.t7[:], ["t7"], ["sgu"])
+        copy("V", T.qs[:], ind(qcur, "sgu", 0, 2 * C), [qcur, (qcur, 1), "sgu"], ["qs"])
+        copy("S", T.sgw[:], ind("cm", "sgu", 0, 2 * C), ["cm", "sgu"], ["sgw"])
+        scan("sc2", "qs", "qs")
+        take("qsu", "sc2")
+        z = "zt"
+        for b in range(4):
+            tt(T[z][:, b:4 * C:4], ind("fh", am, C * b, C * b + C), T.fa[:, C * b:C * b + C], OP.add, [("fh", b), ("fa", b), am], [z])
+        copy("S", T[qnew][:, 0:C], ind("sgw", "qsu"), ["sgw", "qsu"], [qnew])
+        if r < 2:
+            copy("S", T.aw[:], ind(qnew, "pu"), [qnew, "pu"], ["aw"])
+        for b in range(4):
+            copy("S", T.fo[:, C * b:C * b + C], T.pa[:, 512 * b:512 * b + C], [], [("fo", b), ("pa", b)])
+        quant("zc%d" % r, "zs%d" % r, z)
+        for b in range(4):
+            mm(("pa", b), C, "lc", "ls", "zc%d" % r, "zs%d" % r, ["lc", "ls", "zc%d" % r, "zs%d" % r], 128 * b)
+        if r < 2:
+            scan("sc0", "aw", "aw")
+            take("ao%d" % (r + 1), "sc0")
+        else:
+            waits("Y", [qnew], [])
+            dma("Y", [(T.qo[:], T[qnew][0:128:16, 0:C])], "stored", 16, [qnew], [])
+        xn = "xn"
+        for b in range(4):
+            copy("S", T.rs[:, C * b:C * b + C], T.pa[:, 512 * b:512 * b + C], [], [("rs", b), ("pa", b)], 0.03125)
+            tt(T[xn][:, b:4 * C:4], ind("rs", mo, C * b, C * b + C), T.fo[:, C * b:C * b + C], OP.add, [("rs", b), mo, ("fo", b)], [xn])
+        quant("tc%d" % (r + 1), "ts%d" % (r + 1), xn)
+        if r == 0:
+            quant("vc", "vs", "vt")
+        if r < 2:
+            copy("S", T[qnew][:, C:2 * C], ind(qnew, "mu16"), [qnew, "mu16"], [(qnew, 1)])
+        qcur, qnew = qnew, qcur
+    dma("Y", [(T.oc[:], T.tc3[:].bitcast(dt.uint8))] + [(T.osc[4 * k:4 * k + 4, :], T.ts3[32 * k:32 * k + 4, :]) for k in range(4)], "stored", 96, ["tc3", "ts3"], [])
+    mm(("pb", 0), C, "vc", "vs", "tc3", "ts3", ["vc", "vs", "tc3", "ts3"], 0)
+    copy("V", T.yo[:], T.pb[:, 0:C], [], ["yo", ("pb", 0)])
+    dma("Y", [(T.y[:], T.yo[:])], "stored", 112, ["yo"], [])
+    g.sync.wait_ge(T.sem.stored, 112)
+    g.wait_ge(T.sem.sent, sent[0])
+    for q in ("V", "S", "T", "G"):
+        need("G", "q" + q, count[q])
+    for n, t in (("x", 16), ("u", 16), ("v", 16), ("wc", 16), ("ws", 16), ("pl", 16), ("ml", 16), ("qw", 256), ("mw", 256)):
+        need("G", "ld_" + n, t)

@@ -10,60 +10,54 @@ SLOPE, SHIFT = 164, -51997
 UNMET = 162
 NCELL = 53000
 
+
+def wide(*names):
+    return {n: ("sbuf", [128, C], "float32") for n in names}
+
+
+def double(*names):
+    return {n: ("sbuf", [128, 2 * C], "float32") for n in names}
+
+
+def small(d, *names):
+    return {n: ("sbuf", [128, K], d) for n in names}
+
+
+def column(d, *names):
+    return {n: ("sbuf", [128, 1], d) for n in names}
+
+
+def tiles(*names):
+    return {n: ("sbuf", [128, 4 * C], "bfloat16") for n in names}
+
+
+def codes(n, *pairs):
+    d = {}
+    for c, s in pairs:
+        d[c] = ("sbuf", [128, n], "float8_e4m3fn_x4")
+        d[s] = ("sbuf", [128, n], "uint8")
+    return d
+
+
 SCRATCH = {
-    "x0": ("sbuf", [128, 4 * C], "bfloat16"), "xn": ("sbuf", [128, 4 * C], "bfloat16"), "zt": ("sbuf", [128, 4 * C], "bfloat16"), "ut": ("sbuf", [128, 512], "bfloat16"), "vt": ("sbuf", [128, 512], "bfloat16"),
-    "uc": ("sbuf", [128, 128], "float8_e4m3fn_x4"), "us": ("sbuf", [128, 128], "uint8"),
-    "urc": ("sbuf", [128, 128], "float8_e4m3fn_x4"), "urs": ("sbuf", [128, 128], "uint8"),
-    "vc": ("sbuf", [128, 128], "float8_e4m3fn_x4"), "vs": ("sbuf", [128, 128], "uint8"),
-    "lc": ("sbuf", [128, 512], "float8_e4m3fn_x4"), "ls": ("sbuf", [128, 512], "uint8"),
-    "ec": ("sbuf", [128, 512], "float8_e4m3fn_x4"), "es": ("sbuf", [128, 512], "uint8"),
+    **tiles("x0", "xn", "zt", "fo", "fh", "fa"),
+    "ut": ("sbuf", [128, 512], "bfloat16"), "vt": ("sbuf", [128, 512], "bfloat16"),
+    **codes(128, ("uc", "us"), ("urc", "urs"), ("vc", "vs")), **codes(512, ("lc", "ls"), ("ec", "es")),
+    **codes(C, *[("zc%d" % r, "zs%d" % r) for r in range(3)], *[("ac%d" % r, "as%d" % r) for r in range(3)], *[("tc%d" % r, "ts%d" % r) for r in range(4)]),
     "eone": ("sbuf", [128, 516], "bfloat16"), "ebase": ("sbuf", [128, 516], "bfloat16"),
-    "qpi": ("sbuf", [128, C], "int32"), "mpi": ("sbuf", [128, C], "int32"),
-    "pli": ("sbuf", [128, K], "int32"), "mli": ("sbuf", [128, K], "int32"),
-    "pu": ("sbuf", [128, K], "uint16"), "mu16": ("sbuf", [128, K], "uint16"),
-    "lowu": ("sbuf", [128, K], "uint16"), "highu": ("sbuf", [128, K], "uint16"),
-    "muf": ("sbuf", [128, K], "float32"), "tlo": ("sbuf", [128, K], "float32"), "thi": ("sbuf", [128, K], "float32"),
-    "ji": ("sbuf", [128, C], "int32"), "ja": ("sbuf", [128, C], "int32"), "jf": ("sbuf", [128, C], "float32"),
-    "md": ("sbuf", [128, C], "float32"),
-    "pi1": ("sbuf", [128, 1], "int32"), "pa1": ("sbuf", [128, 1], "int32"), "pf1": ("sbuf", [128, 1], "float32"),
-    "p20": ("sbuf", [128, 1], "float32"), "qoff": ("sbuf", [128, 1], "float32"),
-    "k16": ("sbuf", [128, K], "int32"), "k1": ("sbuf", [128, K], "int32"), "u8i": ("sbuf", [128, 8], "int32"),
-    "coff": ("sbuf", [128, K], "float32"), "c640": ("sbuf", [128, K], "float32"),
-    "piu": ("sbuf", [128, K], "uint16"), "upick": ("sbuf", [128, 8], "uint16"),
-    "cb": ("sbuf", [128, C], "bfloat16"),
-    "wa": ("sbuf", [128, 2 * C], "float32"), "wb": ("sbuf", [128, 2 * C], "float32"),
-    "d0": ("sbuf", [128, 2 * C], "float32"), "d1": ("sbuf", [128, 2 * C], "float32"), "d2": ("sbuf", [128, 2 * C], "float32"), "d3": ("sbuf", [128, 2 * C], "float32"),
-    "lw": ("sbuf", [128, 3 * C], "float32"), "lg": ("sbuf", [128, C], "float32"),
-    "tab": ("sbuf", [128, NCELL], "bfloat16"),
-    "qq": ("sbuf", [128, 2 * C], "float32"), "qr": ("sbuf", [128, 2 * C], "float32"), "cm": ("sbuf", [128, 2 * C], "float32"),
-    "aw": ("sbuf", [128, C], "float32"), "f320": ("sbuf", [128, C], "float32"), "ssb": ("sbuf", [128, C], "float32"),
-    "sc0": ("sbuf", [128, C], "float32"), "sc1": ("sbuf", [128, C], "float32"), "sc2": ("sbuf", [128, C], "float32"),
-    "nf": ("sbuf", [128, K], "float32"), "nfk": ("sbuf", [128, K], "float32"),
-    "wf": ("sbuf", [128, K], "float32"), "wg": ("sbuf", [128, K], "float32"), "gg": ("sbuf", [128, K], "float32"),
-    "df": ("sbuf", [128, K], "float32"), "t1": ("sbuf", [128, K], "float32"), "t2": ("sbuf", [128, K], "float32"),
-    "t3": ("sbuf", [128, K], "float32"), "t4": ("sbuf", [128, K], "float32"), "t5": ("sbuf", [128, K], "float32"),
-    "t6": ("sbuf", [128, K], "float32"), "t7": ("sbuf", [128, K], "float32"),
-    "wu": ("sbuf", [128, K], "uint16"), "wz": ("sbuf", [128, K], "uint16"), "lu": ("sbuf", [128, K], "uint16"),
-    "k1u": ("sbuf", [128, K], "uint16"), "k2u": ("sbuf", [128, K], "uint16"),
-    "sgu": ("sbuf", [128, K], "uint16"), "qsu": ("sbuf", [128, K], "uint16"),
-    "mw": ("sbuf", [128, C], "float32"), "sm": ("sbuf", [128, C], "float32"), "smh": ("sbuf", [128, C], "float32"),
-    "sw": ("sbuf", [128, C], "float32"), "sgw": ("sbuf", [128, C], "float32"), "qs": ("sbuf", [128, C], "float32"),
-    "fo": ("sbuf", [128, 4 * C], "bfloat16"), "fh": ("sbuf", [128, 4 * C], "bfloat16"), "fa": ("sbuf", [128, 4 * C], "bfloat16"),
-    "rs": ("sbuf", [128, 4 * C], "float32"), "yo": ("sbuf", [128, C], "float32"),
+    "qpi": ("sbuf", [128, C], "int32"), "mpi": ("sbuf", [128, C], "int32"), "ji": ("sbuf", [128, C], "int32"), "ja": ("sbuf", [128, C], "int32"),
+    "u8i": ("sbuf", [128, 8], "int32"), "upick": ("sbuf", [128, 8], "uint16"), "cb": ("sbuf", [128, C], "bfloat16"),
+    "fm": ("sbuf", [128, C], "bfloat16"), "y3": ("sbuf", [128, C], "bfloat16"),
+    **column("int32", "pi1", "pa1"), **column("float32", "pf1", "p20", "qoff", "nqo", "nwg"),
+    **small("int32", "pli", "mli", "k16", "k1"),
+    **small("uint16", "pu", "mu16", "lowu", "highu", "piu", "wu", "wz", "lu", "k1u", "k2u", "sgu", "qsu"),
+    **small("uint16", *["%s%d" % (n, r) for n in ("am", "aa", "mo", "ao") for r in range(3)]),
+    **small("float32", "coff", "c640", "nf", "nfk", "wf", "wg", "gg", "df", "t1", "t2", "t3", "t4", "t5", "t6"),
+    **wide("jf", "md", "lg", "aw", "f320", "ssb", "sc0", "sc1", "sc2", "mw", "sm", "smh", "sw", "sgw", "qs", "yo"),
+    **double("wa", "wb", "d1", "d2", "d3", "qq", "qr", "cm"),
+    "lw": ("sbuf", [128, 3 * C], "float32"), "tab": ("sbuf", [128, NCELL], "bfloat16"), "rs": ("sbuf", [128, 3 * C], "float32"),
     "pa": ("psum", [128, 2048], "float32"), "pb": ("psum", [128, 2048], "float32"),
 }
-for _r in range(3):
-    SCRATCH["zc%d" % _r] = ("sbuf", [128, C], "float8_e4m3fn_x4")
-    SCRATCH["zs%d" % _r] = ("sbuf", [128, C], "uint8")
-    SCRATCH["ac%d" % _r] = ("sbuf", [128, C], "float8_e4m3fn_x4")
-    SCRATCH["as%d" % _r] = ("sbuf", [128, C], "uint8")
-    SCRATCH["am%d" % _r] = ("sbuf", [128, K], "uint16")
-    SCRATCH["aa%d" % _r] = ("sbuf", [128, K], "uint16")
-    SCRATCH["mo%d" % _r] = ("sbuf", [128, K], "uint16")
-    SCRATCH["ao%d" % _r] = ("sbuf", [128, K], "uint16")
-for _r in range(4):
-    SCRATCH["tc%d" % _r] = ("sbuf", [128, C], "float8_e4m3fn_x4")
-    SCRATCH["ts%d" % _r] = ("sbuf", [128, C], "uint8")
 
 SEMAPHORES = ["qV", "qS", "qT", "qG", "sent", "stored"] + ["ld_" + n for n in ("x", "u", "v", "wc", "ws", "pl", "ml", "qw", "mw")]
 for _r in range(3):
@@ -146,14 +140,10 @@ def rank_program(g, core, T, topo):
     op, dma, arrives, waits, need, count = make_queues(g, T)
     sent = [0]
 
-    def A(name, a=0, b=None):
-        return T[name][:, a:b] if b is not None else T[name][:]
-
     def send(dst, out, in_, sem, key):
         waits("G", [key], [])
         rid, pid, _ = topo.addr(dst)
-        m = topo.mask(core, dst)
-        g.remote_dma(out, in_, T.sem[sem], T.sem.sent, pid, rid, m)
+        g.remote_dma(out, in_, T.sem[sem], T.sem.sent, pid, rid, topo.mask(core, dst))
         sent[0] += len(topo.engines(core, dst))
 
     def copy(q, out, in_, reads, writes, scale=None):
@@ -174,11 +164,14 @@ def rank_program(g, core, T, topo):
         else:
             op("V", lambda e: e.tensor_scalar(out, a, s1, s2, o1, o2), reads, writes)
 
+    def fill(ap, value, key):
+        op("V", lambda e: e.memset(ap, value), [], [key])
+
     def ind(win, off, a=0, b=C):
         return T[win][:, a:b].indirect(T[off][:, 0:K])
 
-    def scan(dst, src, key):
-        op("V", lambda e: e.tensor_tensor_scan(T[dst][:], T.md[:], T[src][:, 0:C], 0.0, OP.add, OP.max), ["md", key], [dst])
+    def scan(dst, src):
+        op("V", lambda e: e.tensor_tensor_scan(T[dst][:], T.md[:], T[src][:, 0:C], 0.0, OP.add, OP.max), ["md", src], [dst])
 
     def ends(sc):
         return T[sc][:, 15:C:16]
@@ -186,17 +179,23 @@ def rank_program(g, core, T, topo):
     def take(out, sc, extra=None, o=None):
         ts(T[out][:], ends(sc), T.qoff[:, 0:1], OP.subtract, [sc, "qoff"], [out], extra, o)
 
-    def mm(bank, n, lc, ls, rc, rs, reads, a):
+    def mm(bank, lc, ls, rc, rs, reads, a):
         buf, b = bank
-        op("T", lambda e: e.matmul_mx(T[buf][:, 512 * b:512 * b + n], T[lc][:, a:a + 128], T[ls][:, a:a + 128], T[rc][:], T[rs][:], True, True), reads, [(buf, b)])
+        op("T", lambda e: e.matmul_mx(T[buf][:, 512 * b:512 * b + C], T[lc][:, a:a + 128], T[ls][:, a:a + 128], T[rc][:], T[rs][:], True, True), reads, [(buf, b)])
 
-    dma("S", [(T.x0[:], T.x[:])], "ld_x", 16, [], ["x0"])
+    def quant(c, s, t, keys=None):
+        op("V", lambda e: e.quantize_mx(T[c][:], T[s][:], T[t][:]), keys or [t], [c, s])
+
+    def unit(b):
+        op("V", lambda e: e.quantize_mx(T.ec[:, 128 * b:128 * b + 128], T.es[:, 128 * b:128 * b + 128], T.ebase[:, 3 - b:515 - b]), ["ebase"], [("ec", b)])
+
     dma("S", [(T.ut[:], T.u[:])], "ld_u", 16, [], ["ut"])
-    dma("Y", [(T.pli[:], T.pl[:])], "ld_pl", 16, [], ["pli"])
+    dma("S", [(T.x0[:], T.x[:])], "ld_x", 16, [], ["x0"])
+    dma("S", [(T.pli[:], T.pl[:])], "ld_pl", 16, [], ["pli"])
+    dma("S", [(T.mli[:], T.ml[:])], "ld_ml", 16, [], ["mli"])
     dma("Y", [(T.qpi[i:128:16, :], T.ql[:]) for i in range(16)], "ld_qw", 256, [], ["qpi"])
     dma("S", [(T.lc[:].bitcast(dt.uint8), T.wc[:])], "ld_wc", 16, [], ["lc"])
     dma("S", [(T.ls[:], T.ws[:])], "ld_ws", 16, [], ["ls"])
-    dma("Y", [(T.mli[:], T.ml[:])], "ld_ml", 16, [], ["mli"])
     dma("Y", [(T.mpi[i:128:16, :], T.ml[:]) for i in range(16)], "ld_mw", 256, [], ["mpi"])
     dma("Y", [(T.vt[:], T.v[:])], "ld_v", 16, [], ["vt"])
     for r in range(3):
@@ -209,68 +208,75 @@ def rank_program(g, core, T, topo):
         op("G", lambda e: e.iota(T[name][:, a:b], [[step, b - a]], base, mult, allow_small_or_imprecise_dtypes=True) if flag else e.iota(T[name][:, a:b], [[step, b - a]], base, mult), [], [name])
     iota("pi1", 0, 1, 1, 0, 1)
     iota("ji", 0, C, 1, 4096, -1)
+    iota("u8i", 0, 8, 16, 0, 0)
     iota("k1", 0, K, 1, 0, 0)
     iota("k16", 0, K, 16, 0, 0)
-    iota("u8i", 0, 8, 16, 0, 0)
-    op("V", lambda e: e.memset(T.eone[:], 1.0), [], ["eone"])
+    fill(T.eone[:], 1.0, "eone")
     op("G", lambda e: e.affine_select(T.ebase[:], T.eone[:], [[-1, 516]], OP.is_equal, 0.0, 3, 4), ["eone"], ["ebase"])
     iota("wa", C, 2 * C, 1, C, 0, True)
     iota("wb", C, 2 * C, 1, C, 0, True)
     iota("cb", 0, C, 1, -160, 0, True)
     iota("cm", 0, C, 1, 0, 0, True)
     ts(T.pa1[:], T.pi1[:], 15, OP.bitwise_and, ["pi1"], ["pa1"])
+    fill(T.d1[:, C:2 * C], 0.0, "d1")
     ts(T.pf1[:], T.pa1[:], 1.0, OP.mult, ["pa1"], ["pf1"])
     ts(T.ja[:], T.ji[:], 15, OP.bitwise_and, ["ji"], ["ja"])
     ts(T.p20[:], T.pf1[:], 20.0, OP.mult, ["pf1"], ["p20"])
     ts(T.qoff[:], T.pf1[:], -BIG, OP.mult, ["pf1"], ["qoff"], 15 * BIG, OP.add)
+    ts(T.nqo[:], T.pf1[:], BIG, OP.mult, ["pf1"], ["nqo"], -15 * BIG, OP.add)
     ts(T.jf[:], T.ja[:], 0.0, OP.is_equal, ["ja"], ["jf"], -33 * BIG, OP.mult)
+    copy("V", T.upick[:], T.u8i[:], ["u8i"], ["upick"])
     ts(T.piu[:], T.k1[:], T.p20[:, 0:1], OP.add, ["k1", "p20"], ["piu"])
     ts(T.coff[:], T.k16[:], T.pf1[:, 0:1], OP.add, ["k16", "pf1"], ["coff"])
     ts(T.md[:], T.jf[:], BIG, OP.add, ["jf"], ["md"])
+    ts(T.nwg[:], T.nqo[:], float(SLOPE), OP.mult, ["nqo"], ["nwg"], float(SHIFT), OP.add)
     ts(T.c640[:], T.coff[:], float(2 * C), OP.add, ["coff"], ["c640"])
-    copy("V", T.upick[:], T.u8i[:], ["u8i"], ["upick"])
-    op("V", lambda e: e.memset(T.d0[:, 0:C], 1.0), [], ["d0"])
-    op("V", lambda e: e.memset(T.d0[:, C:2 * C], 0.0), [], ["d0"])
-    for n in ("d1", "d2", "d3"):
-        op("V", (lambda n: lambda e: e.memset(T[n][:, C:2 * C], 0.0))(n), [], [n])
-    op("V", lambda e: e.memset(T.lw[:], float(2 * UNMET)), [], ["lw"])
-
-    def quant(c, s, t, a=0, b=None, ca=0, cb=None):
-        cv = T[c][:, ca:cb] if cb else T[c][:]
-        sv = T[s][:, ca:cb] if cb else T[s][:]
-        tv = T[t][:, a:b] if b else T[t][:]
-        op("V", lambda e: e.quantize_mx(cv, sv, tv), [t], [c, s])
-
-    for b in range(4):
-        quant("ec", "es", "ebase", 3 - b, 3 - b + 512, 128 * b, 128 * b + 128)
     copy("V", T.pu[:], T.pli[:], ["pli"], ["pu"])
-    copy("V", T.qq[:, 0:C], ind("qpi", "piu"), ["qpi", "piu"], ["qq"])
-    copy("V", T.aw[:], ind("qq", "pu"), ["qq", "pu"], ["aw"])
-    scan("sc0", "aw", "aw")
-    take("ao0", "sc0")
+    fill(T.lw[:, 0:C], float(2 * UNMET), "lw")
+    for n in ("d2", "d3"):
+        copy("S", T[n][:, C:2 * C], T.d1[:, C:2 * C], ["d1"], [n])
+
     quant("uc", "us", "ut")
-    op("V", lambda e: e.tensor_copy(T.urc[:].bitcast(dt.uint32), T.uc[:].bitcast(dt.uint32).indirect(T.upick[:, 0:8])), ["uc", "upick"], ["urc"])
+    unit(0)
     op("S", lambda e: e.activation(T.urs[:], T.us[:].indirect(T.upick[:, 0:8]), AF.Copy), ["us", "upick"], ["urs"])
+    op("V", lambda e: e.tensor_copy(T.urc[:].bitcast(dt.uint32), T.uc[:].bitcast(dt.uint32).indirect(T.upick[:, 0:8])), ["uc", "upick"], ["urc"])
     quant("tc0", "ts0", "x0")
+    copy("V", T.qq[:, 0:C], ind("qpi", "piu"), ["qpi", "piu"], ["qq"])
+    unit(1)
+    copy("V", T.aw[:], ind("qq", "pu"), ["qq", "pu"], ["aw"])
 
     qcur, qnew = "qq", "qr"
     for r in range(3):
         partner = T.cores[rank ^ STEP[r]]
-        tc, tsn = "tc%d" % r, "ts%d" % r
+        tc, tsn, zc, zs = "tc%d" % r, "ts%d" % r, "zc%d" % r, "zs%d" % r
         ao, mo, aa, am, ac, asn = "ao%d" % r, "mo%d" % r, "aa%d" % r, "am%d" % r, "ac%d" % r, "as%d" % r
         send(partner, T[ac][:].bitcast(dt.uint8), T[tc][:].bitcast(dt.uint8), "arX%d" % r, tc)
         send(partner, T[asn][:], T[tsn][:], "arX%d" % r, tsn)
-        send(partner, T[aa][:], T[ao][:], "arA%d" % r, ao)
-        mm(("pb", 0), C, "urc", "urs", tc, tsn, ["urc", "urs", tc, tsn], 0)
-        for b in range(4):
-            mm(("pa", b), C, "ec", "es", tc, tsn, ["ec", "es", tc, tsn], 128 * b)
+        mm(("pb", 0), "urc", "urs", tc, tsn, ["urc", "urs", tc, tsn], 0)
         ts(T.f320[:], T.pb[:, 0:C], 0.0, OP.is_lt, [], ["f320", ("pb", 0)], float(C), OP.mult)
-        tt(T.wa[:, 0:C], ind("f320", ao), T.aw[:], OP.add, ["f320", ao, "aw"], ["wa"])
         copy("S", T.ssb[:], T.pb[:, 0:C], [], ["ssb", ("pb", 0)])
+        if r == 0:
+            scan("sc0", "aw")
+            unit(2)
+            take("ao0", "sc0")
+            unit(3)
+        send(partner, T[aa][:], T[ao][:], "arA%d" % r, ao)
+        tt(T.wa[:, 0:C], ind("f320", ao), T.aw[:], OP.add, ["f320", ao, "aw"], ["wa"])
         for b in range(4):
-            mm(("pb", b), C, "ec", "es", ac, asn, ["ec", "es", ac, asn], 128 * b)
-        scan("sc0", "wa", "wa")
+            mm(("pa", b), "ec", "es", tc, tsn, [("ec", b), tc, tsn], 128 * b)
+        for b in range(4):
+            mm(("pb", b), "ec", "es", ac, asn, [("ec", b), ac, asn], 128 * b)
+        if r == 0:
+            copy("V", T.gg[:], T.mli[:], ["mli"], ["gg"])
+            copy("V", T.mu16[:], T.mli[:], ["mli"], ["mu16"])
+        scan("sc0", "wa")
+        if r == 0:
+            tt(T.wf[:], T.gg[:], T.coff[:], OP.min, ["gg", "coff"], ["wf"])
+            tt(T.wg[:], T.gg[:], T.coff[:], OP.max, ["gg", "coff"], ["wg"])
         take("wu", "sc0")
+        if r == 0:
+            copy("V", T.lowu[:], T.wf[:], ["wf"], ["lowu"])
+            copy("V", T.highu[:], T.wg[:], ["wg"], ["highu"])
 
         def half(b):
             copy("S", T.fh[:, C * b:C * b + C], T.pb[:, 512 * b:512 * b + C], [], [("fh", b), ("pb", b)], 0.5)
@@ -278,116 +284,104 @@ def rank_program(g, core, T, topo):
         def ahead(b):
             copy("S", T.fa[:, C * b:C * b + C], ind("fh", aa, C * b, C * b + C), [("fh", b), aa], [("fa", b)])
 
-        lists = ["wu", "wz"]
-        src, oth = "wa", "wb"
-        dcur, free = "d0", ["d1", "d2", "d3"]
-        for i, k in enumerate(STAGES):
-            lst = lists[i % 2]
-            wsrc, dsrc = src, dcur
-            used = []
-            for j in range(k - 1):
-                dst = oth if wsrc == src else src
-                copy("S", T[dst][:, 0:C], ind(wsrc, lst, 0, 2 * C), [wsrc, lst], [dst])
-                dn = [n for n in free if n != dsrc and n != dcur and n not in used][0]
-                if i == 0:
-                    ts(T[dn][:, 0:C], ind(dsrc, lst, 0, 2 * C), 1.0, OP.add, [dsrc, lst], [dn])
-                else:
-                    tt(T[dn][:, 0:C], ind(dsrc, lst, 0, 2 * C), T.smh[:], OP.add, [dsrc, lst, "smh"], [dn])
-                used.append(dn)
-                wsrc, dsrc = dst, dn
-            if wsrc != src:
-                src, oth = oth, src
-            dcur = dsrc
-            if i < len(STAGES) - 1:
-                copy("S", T.smh[:], T[dcur][:, 0:C], [dcur], ["smh"])
-            if i < len(STAGES) - 1:
-                scan("sc0", src, src)
-                take(lists[(i + 1) % 2], "sc0")
-            if i == 0:
-                scan("sc1", "f320", "f320")
-                ts(T.nf[:], ends("sc1"), T.qoff[:, 0:1], OP.subtract, ["sc1", "qoff"], ["nf"], 0.0, OP.is_equal)
-                tt(T.nfk[:], T.nf[:], T.c640[:], OP.mult, ["nf", "c640"], ["nfk"])
-            if r == 0 and i == 1:
-                copy("V", T.mu16[:], T.mli[:], ["mli"], ["mu16"])
-                copy("V", T.muf[:], T.mli[:], ["mli"], ["muf"])
-                tt(T.tlo[:], T.muf[:], T.coff[:], OP.min, ["muf", "coff"], ["tlo"])
-                tt(T.thi[:], T.muf[:], T.coff[:], OP.max, ["muf", "coff"], ["thi"])
-                copy("V", T.lowu[:], T.tlo[:], ["tlo"], ["lowu"])
-                copy("V", T.highu[:], T.thi[:], ["thi"], ["highu"])
+        copy("S", T.wb[:, 0:C], ind("wa", "wu", 0, 2 * C), ["wa", "wu"], ["wb"])
+        ts(T.d1[:, 0:C], T.wa[:, 0:C], float(C), OP.is_lt, ["wa"], ["d1"], 1.0, OP.add)
+        scan("sc1", "f320")
+        ts(T.d2[:, 0:C], ind("d1", "wu", 0, 2 * C), 1.0, OP.add, ["d1", "wu"], ["d2"])
+        copy("S", T.wa[:, 0:C], ind("wb", "wu", 0, 2 * C), ["wb", "wu"], ["wa"])
+        scan("sc0", "wa")
+        take("wz", "sc0")
+        copy("S", T.smh[:], T.d2[:, 0:C], ["d2"], ["smh"])
+        ts(T.nf[:], ends("sc1"), T.qoff[:, 0:1], OP.subtract, ["sc1", "qoff"], ["nf"], 0.0, OP.is_equal)
+        src, oth, dcur, d_a, d_b = "wa", "wb", "d2", "d3", "d1"
+        lst, nxt = "wz", "wu"
+        for i, k in enumerate(STAGES[1:], 1):
+            copy("S", T[oth][:, 0:C], ind(src, lst, 0, 2 * C), [src, lst], [oth])
+            tt(T[d_a][:, 0:C], ind(dcur, lst, 0, 2 * C), T.smh[:], OP.add, [dcur, lst, "smh"], [d_a])
+            if i == 1:
+                tt(T.t4[:], T.nf[:], T.c640[:], OP.mult, ["nf", "c640"], ["t4"])
+            if k == 3:
+                copy("S", T[src][:, 0:C], ind(oth, lst, 0, 2 * C), [oth, lst], [src])
+                tt(T[d_b][:, 0:C], ind(d_a, lst, 0, 2 * C), T.smh[:], OP.add, [d_a, lst, "smh"], [d_b])
+                copy("S", T.smh[:], T[d_b][:, 0:C], [d_b], ["smh"])
+                scan("sc0", src)
+                if i == 1:
+                    ts(T.nfk[:], T.t4[:], T.qoff[:, 0:1], OP.add, ["t4", "qoff"], ["nfk"])
+                take(nxt, "sc0")
+                lst, nxt = nxt, lst
+                dcur, d_b = d_b, dcur
+            else:
+                src, dcur = oth, d_a
             if i >= 2:
                 half(i - 2)
         half(3)
-        scan("sc0", src, src)
-        take("wf", "sc0")
+        scan("sc0", src)
+        tt(T.t1[:], ends("sc0"), T.nfk[:], OP.max, ["sc0", "nfk"], ["t1"])
+        op("S", lambda e: e.activation(T.wf[:], ends("sc0"), AF.Identity, T.nqo[:, 0:1]), ["sc0", "nqo"], ["wf"])
+        op("S", lambda e: e.activation(T.wg[:], ends("sc0"), AF.Identity, T.nwg[:, 0:1], float(SLOPE)), ["sc0", "nwg"], ["wg"])
         take("wu", "sc0")
-        tt(T.t1[:], T.wf[:], T.nfk[:], OP.max, ["wf", "nfk"], ["t1"])
-        copy("V", T.lu[:], T.t1[:], ["t1"], ["lu"])
-        op("V", (lambda d: lambda e: e.tensor_copy(T.lw[:].indirect(T.lu[:, 0:K]), T[d][:, 0:C]))(dcur), ["lu", dcur], ["lw"])
+        ts(T.lu[:], T.t1[:], T.qoff[:, 0:1], OP.subtract, ["t1", "qoff"], ["lu"])
+        op("V", lambda e: e.tensor_copy(T.lw[:].indirect(T.lu[:, 0:K]), T[dcur][:, 0:C]), ["lu", dcur], ["lw"])
         copy("S", T.lg[:], ind("lw", "wu", 0, 2 * C), ["lw", "wu"], ["lg"])
-        scan("sc1", dcur, dcur)
-        ts(T.wg[:], T.wf[:], float(SLOPE), OP.mult, ["wf"], ["wg"], float(SHIFT), OP.add)
-        take("df", "sc1")
+        scan("sc1", dcur)
         tt(T.gg[:], T.wf[:], T.wg[:], OP.max, ["wf", "wg"], ["gg"])
+        take("df", "sc1")
+        tt(T.t5[:], T.gg[:], ends("sc1"), OP.subtract, ["gg", "sc1"], ["t5"])
         tt(T.t2[:], T.df[:], T.nf[:], OP.mult, ["df", "nf"], ["t2"])
         tt(T.t3[:], T.gg[:], T.t2[:], OP.add, ["gg", "t2"], ["t3"])
-        tt(T.t4[:], T.gg[:], T.df[:], OP.subtract, ["gg", "df"], ["t4"])
+        scan("sc2", "lg")
         copy("V", T.k1u[:], T.t3[:], ["t3"], ["k1u"])
-        ts(T.t5[:], T.t4[:], T.qoff[:, 0:1], OP.subtract, ["t4", "qoff"], ["t5"])
-        op("V", lambda e: e.tensor_copy(T.tab[:].indirect(T.k1u[:, 0:K]), T.cb[:]), ["k1u", "cb"], ["tab"])
-        scan("sc2", "lg", "lg")
         tt(T.t6[:], ends("sc2"), T.t5[:], OP.add, ["sc2", "t5"], ["t6"])
         copy("V", T.k2u[:], T.t6[:], ["t6"], ["k2u"])
+        op("V", lambda e: e.tensor_copy(T.tab[:].indirect(T.k1u[:, 0:K]), T.cb[:]), ["k1u", "cb"], ["tab"])
         ts(T.mw[:], T.tab[:].indirect(T.k2u[:, 0:K]), 160.0, OP.add, ["tab", "k2u"], ["mw"])
-        ahead(0)
-        ahead(1)
-        scan("sc0", "mw", "mw")
+        for b in range(4):
+            ahead(b)
+        scan("sc0", "mw")
         take(mo, "sc0")
         send(partner, T[am][:], T[mo][:], "arM%d" % r, mo)
+        copy("V", T.sm[:], ind("ssb", mo), ["ssb", mo], ["sm"])
+        copy("S", T.fo[:, 3 * C:4 * C], T.pa[:, 1536:1536 + C], [], [("fo", 3), ("pa", 3)], 32.0)
+        copy("S", T.smh[:], ind("sm", "highu"), ["sm", "highu"], ["smh"])
         if r == 0:
             copy("V", T.cm[:, C:2 * C], ind("mpi", "piu"), ["mpi", "piu"], ["cm"])
-            copy("V", T.qq[:, C:2 * C], ind("qq", "mu16"), ["qq", "mu16"], [("qq", 1)])
-        copy("V", T.sm[:], ind("ssb", mo), ["ssb", mo], ["sm"])
-        ahead(2)
-        copy("S", T.smh[:], ind("sm", "highu"), ["sm", "highu"], ["smh"])
+            copy("S", T.qq[:, C:2 * C], ind("qq", "mu16"), ["qq", "mu16"], [("qq", 1)])
+        if r == 1:
+            quant("vc", "vs", "vt")
         tt(T.sw[:], ind("sm", "lowu"), T.smh[:], OP.is_gt, ["sm", "lowu", "smh"], ["sw"])
-        ahead(3)
-        scan("sc1", "sw", "sw")
-        take("t7", "sc1", float(C), OP.mult)
-        tt(T.t7[:], T.t7[:], T.coff[:], OP.add, ["t7", "coff"], ["t7"])
-        copy("V", T.sgu[:], T.t7[:], ["t7"], ["sgu"])
-        copy("V", T.qs[:], ind(qcur, "sgu", 0, 2 * C), [qcur, (qcur, 1), "sgu"], ["qs"])
+        copy("S", T.fm[:], ind("fo", mo, 3 * C, 4 * C), [("fo", 3), mo], ["fm"])
+        scan("sc1", "sw")
+        take("t1", "sc1", float(C), OP.mult)
+        tt(T.t2[:], T.t1[:], T.coff[:], OP.add, ["t1", "coff"], ["t2"])
+        copy("V", T.sgu[:], T.t2[:], ["t2"], ["sgu"])
+        copy("S", T.qs[:], ind(qcur, "sgu", 0, 2 * C), [qcur, (qcur, 1), "sgu"], ["qs"])
         copy("S", T.sgw[:], ind("cm", "sgu", 0, 2 * C), ["cm", "sgu"], ["sgw"])
-        scan("sc2", "qs", "qs")
-        take("qsu", "sc2")
-        z = "zt"
         for b in range(4):
-            tt(T[z][:, b:4 * C:4], ind("fh", am, C * b, C * b + C), T.fa[:, C * b:C * b + C], OP.add, [("fh", b), ("fa", b), am], [z])
+            tt(T.zt[:, b:4 * C:4], ind("fh", am, C * b, C * b + C), T.fa[:, C * b:C * b + C], OP.add, [("fh", b), ("fa", b), am], [("zt", b)])
+        for b in range(3):
+            copy("S", T.fo[:, C * b:C * b + C], T.pa[:, 512 * b:512 * b + C], [], [("fo", b), ("pa", b)])
+        quant(zc, zs, "zt", [("zt", b) for b in range(4)])
+        for b in (3, 0, 1, 2):
+            mm(("pa", b), "lc", "ls", zc, zs, ["lc", "ls", zc, zs], 128 * b)
+        scan("sc2", "qs")
+        take("qsu", "sc2")
+        tt(T.y3[:], T.pa[:, 1536:1536 + C], T.fm[:], OP.add, ["fm"], ["y3", ("pa", 3)])
+        for b in range(3):
+            copy("S", T.rs[:, C * b:C * b + C], T.pa[:, 512 * b:512 * b + C], [], [("rs", b), ("pa", b)], 0.03125)
+            tt(T.xn[:, b:4 * C:4], ind("rs", mo, C * b, C * b + C), T.fo[:, C * b:C * b + C], OP.add, [("rs", b), mo, ("fo", b)], [("xn", b)])
+        copy("S", T.xn[:, 3:4 * C:4], ind("y3", mo), ["y3", mo], [("xn", 3)], 0.03125)
         copy("S", T[qnew][:, 0:C], ind("sgw", "qsu"), ["sgw", "qsu"], [qnew])
+        quant("tc%d" % (r + 1), "ts%d" % (r + 1), "xn", [("xn", b) for b in range(4)])
         if r < 2:
             copy("S", T.aw[:], ind(qnew, "pu"), [qnew, "pu"], ["aw"])
-        for b in range(4):
-            copy("S", T.fo[:, C * b:C * b + C], T.pa[:, 512 * b:512 * b + C], [], [("fo", b), ("pa", b)])
-        quant("zc%d" % r, "zs%d" % r, z)
-        for b in range(4):
-            mm(("pa", b), C, "lc", "ls", "zc%d" % r, "zs%d" % r, ["lc", "ls", "zc%d" % r, "zs%d" % r], 128 * b)
-        if r < 2:
-            scan("sc0", "aw", "aw")
+            scan("sc0", "aw")
             take("ao%d" % (r + 1), "sc0")
-        else:
-            waits("Y", [qnew], [])
-            dma("Y", [(T.qo[:], T[qnew][0:128:16, 0:C])], "stored", 16, [qnew], [])
-        xn = "xn"
-        for b in range(4):
-            copy("S", T.rs[:, C * b:C * b + C], T.pa[:, 512 * b:512 * b + C], [], [("rs", b), ("pa", b)], 0.03125)
-            tt(T[xn][:, b:4 * C:4], ind("rs", mo, C * b, C * b + C), T.fo[:, C * b:C * b + C], OP.add, [("rs", b), mo, ("fo", b)], [xn])
-        quant("tc%d" % (r + 1), "ts%d" % (r + 1), xn)
-        if r == 0:
-            quant("vc", "vs", "vt")
-        if r < 2:
             copy("S", T[qnew][:, C:2 * C], ind(qnew, "mu16"), [qnew, "mu16"], [(qnew, 1)])
+        else:
+            dma("Y", [(T.qo[:], T[qnew][0:128:16, 0:C])], "stored", 16, [qnew], [])
         qcur, qnew = qnew, qcur
     dma("Y", [(T.oc[:], T.tc3[:].bitcast(dt.uint8))] + [(T.osc[4 * k:4 * k + 4, :], T.ts3[32 * k:32 * k + 4, :]) for k in range(4)], "stored", 96, ["tc3", "ts3"], [])
-    mm(("pb", 0), C, "vc", "vs", "tc3", "ts3", ["vc", "vs", "tc3", "ts3"], 0)
+    mm(("pb", 0), "vc", "vs", "tc3", "ts3", ["vc", "vs", "tc3", "ts3"], 0)
     copy("V", T.yo[:], T.pb[:, 0:C], [], ["yo", ("pb", 0)])
     dma("Y", [(T.y[:], T.yo[:])], "stored", 112, ["yo"], [])
     g.sync.wait_ge(T.sem.stored, 112)

@@ -7,6 +7,7 @@ STEP = [1, 2, 4]
 STAGES = [3, 3, 3, 3, 2]
 BIG = 1024.0
 SLOPE, SHIFT = 164, -51997
+HALF = 512
 UNMET = 162
 NCELL = 53000
 
@@ -47,14 +48,14 @@ SCRATCH = {
     "eone": ("sbuf", [128, 516], "bfloat16"), "ebase": ("sbuf", [128, 516], "bfloat16"),
     "qpi": ("sbuf", [128, C], "int32"), "mpi": ("sbuf", [128, C], "int32"), "ji": ("sbuf", [128, C], "int32"), "ja": ("sbuf", [128, C], "int32"),
     "u8i": ("sbuf", [128, 8], "int32"), "upick": ("sbuf", [128, 8], "uint16"), "cb": ("sbuf", [128, C], "bfloat16"),
-    "fm": ("sbuf", [128, C], "bfloat16"), "y3": ("sbuf", [128, C], "bfloat16"),
-    **column("int32", "pi1", "pa1"), **column("float32", "pf1", "p20", "qoff", "nqo", "nwg"),
+    "fm": ("sbuf", [128, 2 * C], "bfloat16"), "y3": ("sbuf", [128, 2 * C], "bfloat16"),
+    **column("int32", "pi1", "pa1"), **column("float32", "pf1", "p20", "qoff", "nqo", "nwg", "nqh"),
     **small("int32", "pli", "mli", "k16", "k1"),
-    **small("uint16", "pu", "mu16", "lowu", "highu", "piu", "wu", "wz", "lu", "k1u", "k2u", "sgu", "qsu"),
+    **small("uint16", "pu", "mu16", "lowu", "highu", "piu", "ppu", "qpu", "wu", "wz", "lu", "k1u", "k2u", "sgu", "qsu"),
     **small("uint16", *["%s%d" % (n, r) for n in ("am", "aa", "mo", "ao") for r in range(3)]),
-    **small("float32", "coff", "c640", "nf", "nfk", "wf", "wg", "gg", "df", "t1", "t2", "t3", "t4", "t5", "t6"),
-    **wide("jf", "md", "lg", "aw", "f320", "ssb", "sc0", "sc1", "sc2", "mw", "sm", "smh", "sw", "sgw", "qs", "yo"),
-    **double("wa", "wb", "d1", "d2", "d3", "qq", "qr", "cm"),
+    **small("float32", "coff", "c640", "chalf", "nf", "nfk", "wf", "wg", "gg", "df", "t1", "t2", "t3", "t4", "t5"),
+    **wide("md", "lg", "aw", "f320", "ssb", "sc0", "sc1", "sc2", "mw", "sm", "smh", "sw", "sgw", "qs"),
+    **double("wa", "wb", "d1", "d2", "d3"), **{n: ("sbuf", [128, HALF + C], "float32") for n in ("qq", "qr", "cm")},
     "lw": ("sbuf", [128, 3 * C], "float32"), "tab": ("sbuf", [128, NCELL], "bfloat16"), "rs": ("sbuf", [128, 3 * C], "float32"),
     "pa": ("psum", [128, 2048], "float32"), "pb": ("psum", [128, 2048], "float32"),
 }
@@ -194,8 +195,9 @@ def rank_program(g, core, T, topo):
     dma("S", [(T.pli[:], T.pl[:])], "ld_pl", 16, [], ["pli"])
     dma("S", [(T.mli[:], T.ml[:])], "ld_ml", 16, [], ["mli"])
     dma("Y", [(T.qpi[i:128:16, :], T.ql[:]) for i in range(16)], "ld_qw", 256, [], ["qpi"])
-    dma("S", [(T.lc[:].bitcast(dt.uint8), T.wc[:])], "ld_wc", 16, [], ["lc"])
-    dma("S", [(T.ls[:], T.ws[:])], "ld_ws", 16, [], ["ls"])
+    need("Y", "ld_x", 16)
+    dma("Y", [(T.lc[:].bitcast(dt.uint8), T.wc[:])], "ld_wc", 16, [], ["lc"])
+    dma("Y", [(T.ls[:], T.ws[:])], "ld_ws", 16, [], ["ls"])
     dma("Y", [(T.mpi[i:128:16, :], T.ml[:]) for i in range(16)], "ld_mw", 256, [], ["mpi"])
     dma("Y", [(T.vt[:], T.v[:])], "ld_v", 16, [], ["vt"])
     for r in range(3):
@@ -224,26 +226,39 @@ def rank_program(g, core, T, topo):
     ts(T.p20[:], T.pf1[:], 20.0, OP.mult, ["pf1"], ["p20"])
     ts(T.qoff[:], T.pf1[:], -BIG, OP.mult, ["pf1"], ["qoff"], 15 * BIG, OP.add)
     ts(T.nqo[:], T.pf1[:], BIG, OP.mult, ["pf1"], ["nqo"], -15 * BIG, OP.add)
-    ts(T.jf[:], T.ja[:], 0.0, OP.is_equal, ["ja"], ["jf"], -33 * BIG, OP.mult)
+    ts(T.sc2[:], T.ja[:], 0.0, OP.is_equal, ["ja"], ["sc2"], -33 * BIG, OP.mult)
     copy("V", T.upick[:], T.u8i[:], ["u8i"], ["upick"])
     ts(T.piu[:], T.k1[:], T.p20[:, 0:1], OP.add, ["k1", "p20"], ["piu"])
     ts(T.coff[:], T.k16[:], T.pf1[:, 0:1], OP.add, ["k16", "pf1"], ["coff"])
-    ts(T.md[:], T.jf[:], BIG, OP.add, ["jf"], ["md"])
+    ts(T.md[:], T.sc2[:], BIG, OP.add, ["sc2"], ["md"])
     ts(T.nwg[:], T.nqo[:], float(SLOPE), OP.mult, ["nqo"], ["nwg"], float(SHIFT), OP.add)
     ts(T.c640[:], T.coff[:], float(2 * C), OP.add, ["coff"], ["c640"])
+    ts(T.chalf[:], T.coff[:], 1.0 / HALF, OP.mult, ["coff"], ["chalf"])
+    ts(T.nqh[:], T.nqo[:], float(HALF), OP.mult, ["nqo"], ["nqh"])
+    ts(T.k16[:], T.pli[:], 15, OP.bitwise_and, ["pli"], ["k16"])
+    ts(T.k1[:], T.pli[:], 4, OP.arith_shift_right, ["pli"], ["k1"])
     copy("V", T.pu[:], T.pli[:], ["pli"], ["pu"])
+    ts(T.t1[:], T.k16[:], 20.0, OP.mult, ["k16"], ["t1"])
     fill(T.lw[:, 0:C], float(2 * UNMET), "lw")
     for n in ("d2", "d3"):
         copy("S", T[n][:, C:2 * C], T.d1[:, C:2 * C], ["d1"], [n])
 
+    tt(T.t2[:], T.t1[:], T.k1[:], OP.add, ["t1", "k1"], ["t2"])
     quant("uc", "us", "ut")
-    unit(0)
+    copy("V", T.ppu[:], T.t2[:], ["t2"], ["ppu"])
     op("S", lambda e: e.activation(T.urs[:], T.us[:].indirect(T.upick[:, 0:8]), AF.Copy), ["us", "upick"], ["urs"])
     op("V", lambda e: e.tensor_copy(T.urc[:].bitcast(dt.uint32), T.uc[:].bitcast(dt.uint32).indirect(T.upick[:, 0:8])), ["uc", "upick"], ["urc"])
+    copy("V", T.gg[:], T.mli[:], ["mli"], ["gg"])
+    copy("V", T.mu16[:], T.mli[:], ["mli"], ["mu16"])
+    tt(T.wf[:], T.gg[:], T.coff[:], OP.min, ["gg", "coff"], ["wf"])
+    tt(T.wg[:], T.gg[:], T.coff[:], OP.max, ["gg", "coff"], ["wg"])
     quant("tc0", "ts0", "x0")
-    copy("V", T.qq[:, 0:C], ind("qpi", "piu"), ["qpi", "piu"], ["qq"])
-    unit(1)
-    copy("V", T.aw[:], ind("qq", "pu"), ["qq", "pu"], ["aw"])
+    copy("V", T.lowu[:], T.wf[:], ["wf"], ["lowu"])
+    copy("V", T.highu[:], T.wg[:], ["wg"], ["highu"])
+    copy("S", T.aw[:], ind("qpi", "ppu"), ["qpi", "ppu"], ["aw"])
+    copy("S", T.qq[:, 0:C], ind("qpi", "piu"), ["qpi", "piu"], ["qq"])
+    unit(0)
+    scan("sc0", "aw")
 
     qcur, qnew = "qq", "qr"
     for r in range(3):
@@ -255,28 +270,20 @@ def rank_program(g, core, T, topo):
         mm(("pb", 0), "urc", "urs", tc, tsn, ["urc", "urs", tc, tsn], 0)
         ts(T.f320[:], T.pb[:, 0:C], 0.0, OP.is_lt, [], ["f320", ("pb", 0)], float(C), OP.mult)
         copy("S", T.ssb[:], T.pb[:, 0:C], [], ["ssb", ("pb", 0)])
+        take(ao, "sc0")
         if r == 0:
-            scan("sc0", "aw")
-            unit(2)
-            take("ao0", "sc0")
-            unit(3)
+            unit(1)
         send(partner, T[aa][:], T[ao][:], "arA%d" % r, ao)
         tt(T.wa[:, 0:C], ind("f320", ao), T.aw[:], OP.add, ["f320", ao, "aw"], ["wa"])
+        scan("sc0", "wa")
+        take("wu", "sc0")
+        if r == 0:
+            unit(2)
+            unit(3)
         for b in range(4):
             mm(("pa", b), "ec", "es", tc, tsn, [("ec", b), tc, tsn], 128 * b)
         for b in range(4):
             mm(("pb", b), "ec", "es", ac, asn, [("ec", b), ac, asn], 128 * b)
-        if r == 0:
-            copy("V", T.gg[:], T.mli[:], ["mli"], ["gg"])
-            copy("V", T.mu16[:], T.mli[:], ["mli"], ["mu16"])
-        scan("sc0", "wa")
-        if r == 0:
-            tt(T.wf[:], T.gg[:], T.coff[:], OP.min, ["gg", "coff"], ["wf"])
-            tt(T.wg[:], T.gg[:], T.coff[:], OP.max, ["gg", "coff"], ["wg"])
-        take("wu", "sc0")
-        if r == 0:
-            copy("V", T.lowu[:], T.wf[:], ["wf"], ["lowu"])
-            copy("V", T.highu[:], T.wg[:], ["wg"], ["highu"])
 
         def half(b):
             copy("S", T.fh[:, C * b:C * b + C], T.pb[:, 512 * b:512 * b + C], [], [("fh", b), ("pb", b)], 0.5)
@@ -312,28 +319,29 @@ def rank_program(g, core, T, topo):
                 dcur, d_b = d_b, dcur
             else:
                 src, dcur = oth, d_a
-            if i >= 2:
-                half(i - 2)
-        half(3)
+        half(0)
+        half(1)
         scan("sc0", src)
+        scan("sc1", dcur)
         tt(T.t1[:], ends("sc0"), T.nfk[:], OP.max, ["sc0", "nfk"], ["t1"])
         op("S", lambda e: e.activation(T.wf[:], ends("sc0"), AF.Identity, T.nqo[:, 0:1]), ["sc0", "nqo"], ["wf"])
         op("S", lambda e: e.activation(T.wg[:], ends("sc0"), AF.Identity, T.nwg[:, 0:1], float(SLOPE)), ["sc0", "nwg"], ["wg"])
         take("wu", "sc0")
         ts(T.lu[:], T.t1[:], T.qoff[:, 0:1], OP.subtract, ["t1", "qoff"], ["lu"])
-        op("V", lambda e: e.tensor_copy(T.lw[:].indirect(T.lu[:, 0:K]), T[dcur][:, 0:C]), ["lu", dcur], ["lw"])
-        copy("S", T.lg[:], ind("lw", "wu", 0, 2 * C), ["lw", "wu"], ["lg"])
-        scan("sc1", dcur)
-        tt(T.gg[:], T.wf[:], T.wg[:], OP.max, ["wf", "wg"], ["gg"])
         take("df", "sc1")
-        tt(T.t5[:], T.gg[:], ends("sc1"), OP.subtract, ["gg", "sc1"], ["t5"])
+        op("V", lambda e: e.tensor_copy(T.lw[:].indirect(T.lu[:, 0:K]), T[dcur][:, 0:C]), ["lu", dcur], ["lw"])
+        half(2)
+        half(3)
+        copy("S", T.lg[:], ind("lw", "wu", 0, 2 * C), ["lw", "wu"], ["lg"])
         tt(T.t2[:], T.df[:], T.nf[:], OP.mult, ["df", "nf"], ["t2"])
+        tt(T.gg[:], T.wf[:], T.wg[:], OP.max, ["wf", "wg"], ["gg"])
         tt(T.t3[:], T.gg[:], T.t2[:], OP.add, ["gg", "t2"], ["t3"])
-        scan("sc2", "lg")
+        tt(T.t5[:], T.gg[:], ends("sc1"), OP.subtract, ["gg", "sc1"], ["t5"])
         copy("V", T.k1u[:], T.t3[:], ["t3"], ["k1u"])
-        tt(T.t6[:], ends("sc2"), T.t5[:], OP.add, ["sc2", "t5"], ["t6"])
-        copy("V", T.k2u[:], T.t6[:], ["t6"], ["k2u"])
         op("V", lambda e: e.tensor_copy(T.tab[:].indirect(T.k1u[:, 0:K]), T.cb[:]), ["k1u", "cb"], ["tab"])
+        scan("sc2", "lg")
+        tt(T.t4[:], ends("sc2"), T.t5[:], OP.add, ["sc2", "t5"], ["t4"])
+        copy("V", T.k2u[:], T.t4[:], ["t4"], ["k2u"])
         ts(T.mw[:], T.tab[:].indirect(T.k2u[:, 0:K]), 160.0, OP.add, ["tab", "k2u"], ["mw"])
         for b in range(4):
             ahead(b)
@@ -341,49 +349,89 @@ def rank_program(g, core, T, topo):
         take(mo, "sc0")
         send(partner, T[am][:], T[mo][:], "arM%d" % r, mo)
         copy("V", T.sm[:], ind("ssb", mo), ["ssb", mo], ["sm"])
-        copy("S", T.fo[:, 3 * C:4 * C], T.pa[:, 1536:1536 + C], [], [("fo", 3), ("pa", 3)], 32.0)
+        for b in (3, 2):
+            copy("S", T.fo[:, C * b:C * b + C], T.pa[:, 512 * b:512 * b + C], [], [("fo", b), ("pa", b)], 32.0)
+
+        def own(b):
+            copy("S", T.fm[:, C * (b - 2):C * (b - 1)], ind("fo", mo, C * b, C * b + C), [("fo", b), mo], [("fm", b)])
+
+        def early(b):
+            c = C * (b - 2)
+            tt(T.y3[:, c:c + C], T.pa[:, 512 * b:512 * b + C], T.fm[:, c:c + C], OP.add, [("fm", b)], [("y3", b), ("pa", b)])
+
+        def turn(b):
+            copy("S", T.xn[:, b:4 * C:4], ind("y3", mo, C * (b - 2), C * (b - 1)), [("y3", b), mo], [("xn", b)], 0.03125)
+
+        def scaled(b):
+            copy("S", T.rs[:, C * b:C * b + C], T.pa[:, 512 * b:512 * b + C], [], [("rs", b), ("pa", b)], 0.03125)
+
+        def late(b):
+            tt(T.xn[:, b:4 * C:4], ind("rs", mo, C * b, C * b + C), T.fo[:, C * b:C * b + C], OP.add, [("rs", b), mo, ("fo", b)], [("xn", b)])
+
         copy("S", T.smh[:], ind("sm", "highu"), ["sm", "highu"], ["smh"])
         if r == 0:
-            copy("V", T.cm[:, C:2 * C], ind("mpi", "piu"), ["mpi", "piu"], ["cm"])
-            copy("S", T.qq[:, C:2 * C], ind("qq", "mu16"), ["qq", "mu16"], [("qq", 1)])
-        if r == 1:
+            copy("V", T.cm[:, HALF:HALF + C], ind("mpi", "piu"), ["mpi", "piu"], ["cm"])
+            copy("S", T.qq[:, HALF:HALF + C], ind("qq", "mu16"), ["qq", "mu16"], [("qq", 1)])
+        if r == 2:
             quant("vc", "vs", "vt")
         tt(T.sw[:], ind("sm", "lowu"), T.smh[:], OP.is_gt, ["sm", "lowu", "smh"], ["sw"])
-        copy("S", T.fm[:], ind("fo", mo, 3 * C, 4 * C), [("fo", 3), mo], ["fm"])
+        own(3)
         scan("sc1", "sw")
-        take("t1", "sc1", float(C), OP.mult)
-        tt(T.t2[:], T.t1[:], T.coff[:], OP.add, ["t1", "coff"], ["t2"])
-        copy("V", T.sgu[:], T.t2[:], ["t2"], ["sgu"])
-        copy("S", T.qs[:], ind(qcur, "sgu", 0, 2 * C), [qcur, (qcur, 1), "sgu"], ["qs"])
-        copy("S", T.sgw[:], ind("cm", "sgu", 0, 2 * C), ["cm", "sgu"], ["sgw"])
+
+        def sigma():
+            tt(T.t2[:], ends("sc1"), T.chalf[:], OP.add, ["sc1", "chalf"], ["t2"])
+            ts(T.sgu[:], T.t2[:], float(HALF), OP.mult, ["t2", "nqh"], ["sgu"], T.nqh[:, 0:1], OP.add)
+
+        def through():
+            copy("S", T.qs[:], ind(qcur, "sgu", 0, HALF + C), [qcur, (qcur, 1), "sgu"], ["qs"])
+            copy("S", T.sgw[:], ind("cm", "sgu", 0, HALF + C), ["cm", "sgu"], ["sgw"])
+
+        if r < 2:
+            sigma()
+            through()
+            copy("S", T.lg[:], ind("qs", "pu"), ["qs", "pu"], ["lg"])
         for b in range(4):
             tt(T.zt[:, b:4 * C:4], ind("fh", am, C * b, C * b + C), T.fa[:, C * b:C * b + C], OP.add, [("fh", b), ("fa", b), am], [("zt", b)])
-        for b in range(3):
+        own(2)
+        for b in range(2):
             copy("S", T.fo[:, C * b:C * b + C], T.pa[:, 512 * b:512 * b + C], [], [("fo", b), ("pa", b)])
         quant(zc, zs, "zt", [("zt", b) for b in range(4)])
-        for b in (3, 0, 1, 2):
+        for b in (0, 2, 1, 3):
             mm(("pa", b), "lc", "ls", zc, zs, ["lc", "ls", zc, zs], 128 * b)
-        scan("sc2", "qs")
-        take("qsu", "sc2")
-        tt(T.y3[:], T.pa[:, 1536:1536 + C], T.fm[:], OP.add, ["fm"], ["y3", ("pa", 3)])
-        for b in range(3):
-            copy("S", T.rs[:, C * b:C * b + C], T.pa[:, 512 * b:512 * b + C], [], [("rs", b), ("pa", b)], 0.03125)
-            tt(T.xn[:, b:4 * C:4], ind("rs", mo, C * b, C * b + C), T.fo[:, C * b:C * b + C], OP.add, [("rs", b), mo, ("fo", b)], [("xn", b)])
-        copy("S", T.xn[:, 3:4 * C:4], ind("y3", mo), ["y3", mo], [("xn", 3)], 0.03125)
-        copy("S", T[qnew][:, 0:C], ind("sgw", "qsu"), ["sgw", "qsu"], [qnew])
+        if r < 2:
+            scan("sc2", "lg")
+            take("qpu", "sc2")
+        else:
+            sigma()
+        scaled(0)
+        early(2)
+        late(0)
+        scaled(1)
+        turn(2)
+        early(3)
+        late(1)
+        turn(3)
+        if r < 2:
+            copy("S", T.aw[:], ind("sgw", "qpu"), ["sgw", "qpu"], ["aw"])
+        else:
+            through()
         quant("tc%d" % (r + 1), "ts%d" % (r + 1), "xn", [("xn", b) for b in range(4)])
         if r < 2:
-            copy("S", T.aw[:], ind(qnew, "pu"), [qnew, "pu"], ["aw"])
+            scan("sc1", "qs")
             scan("sc0", "aw")
-            take("ao%d" % (r + 1), "sc0")
-            copy("S", T[qnew][:, C:2 * C], ind(qnew, "mu16"), [qnew, "mu16"], [(qnew, 1)])
         else:
-            dma("Y", [(T.qo[:], T[qnew][0:128:16, 0:C])], "stored", 16, [qnew], [])
+            scan("sc1", "qs")
+        take("qsu", "sc1")
+        copy("S", T[qnew][:, 0:C], ind("sgw", "qsu"), ["sgw", "qsu"], [qnew])
+        if r < 2:
+            copy("S", T[qnew][:, HALF:HALF + C], ind(qnew, "mu16"), [qnew, "mu16"], [(qnew, 1)])
+        else:
+            dma("S", [(T.qo[:], T[qnew][0:128:16, 0:C])], "stored", 16, [qnew], [])
         qcur, qnew = qnew, qcur
     dma("Y", [(T.oc[:], T.tc3[:].bitcast(dt.uint8))] + [(T.osc[4 * k:4 * k + 4, :], T.ts3[32 * k:32 * k + 4, :]) for k in range(4)], "stored", 96, ["tc3", "ts3"], [])
     mm(("pb", 0), "vc", "vs", "tc3", "ts3", ["vc", "vs", "tc3", "ts3"], 0)
-    copy("V", T.yo[:], T.pb[:, 0:C], [], ["yo", ("pb", 0)])
-    dma("Y", [(T.y[:], T.yo[:])], "stored", 112, ["yo"], [])
+    copy("V", T.sc2[:], T.pb[:, 0:C], [], ["sc2", ("pb", 0)])
+    dma("Y", [(T.y[:], T.sc2[:])], "stored", 112, ["sc2"], [])
     g.sync.wait_ge(T.sem.stored, 112)
     g.wait_ge(T.sem.sent, sent[0])
     for q in ("V", "S", "T", "G"):

from concourse.bass import DstId, RemoteDMATransfer
from concourse.mybir import dt, AluOpType as OP, ActivationFunctionType as AF

C = 320
K = C // 16
STEP = [1, 2, 4]
STAGES = [3, 3, 3, 3, 2]
BIG = 1024.0
SLOPE, SHIFT = 164, -51997
HALF = 512
UNMET = 162
NCELL = 53000


def wide(*names):
    return {n: ("sbuf", [128, C], "float32") for n in names}


def double(*names):
    return {n: ("sbuf", [128, 2 * C], "float32") for n in names}


def small(d, *names):
    return {n: ("sbuf", [128, K], d) for n in names}


def column(d, *names):
    return {n: ("sbuf", [128, 1], d) for n in names}


def tiles(*names):
    return {n: ("sbuf", [128, 4 * C], "bfloat16") for n in names}


def codes(n, *pairs):
    d = {}
    for c, s in pairs:
        d[c] = ("sbuf", [128, n], "float8_e4m3fn_x4")
        d[s] = ("sbuf", [128, n], "uint8")
    return d


SCRATCH = {
    **tiles("x0", "xn", "zt", "fo", "fh", "fa"),
    "ut": ("sbuf", [128, 512], "bfloat16"), "vt": ("sbuf", [128, 512], "bfloat16"),
    **codes(128, ("uc", "us"), ("urc", "urs"), ("vc", "vs")), **codes(512, ("lc", "ls"), ("ec", "es")),
    **codes(C, *[("zc%d" % r, "zs%d" % r) for r in range(3)], *[("ac%d" % r, "as%d" % r) for r in range(3)], *[("tc%d" % r, "ts%d" % r) for r in range(4)]),
    "eone": ("sbuf", [128, 516], "bfloat16"), "ebase": ("sbuf", [128, 516], "bfloat16"),
    "qpi": ("sbuf", [128, C], "int32"), "mpi": ("sbuf", [128, C], "int32"), "ji": ("sbuf", [128, C], "int32"), "ja": ("sbuf", [128, C], "int32"),
    "u8i": ("sbuf", [128, 8], "int32"), "upick": ("sbuf", [128, 8], "uint16"), "cb": ("sbuf", [128, C], "bfloat16"),
    "fm": ("sbuf", [128, 2 * C], "bfloat16"), "y3": ("sbuf", [128, 2 * C], "bfloat16"),
    **column("int32", "pi1", "pa1"), **column("float32", "pf1", "p20", "qoff", "nqo", "nwg", "nqh"),
    **small("int32", "pli", "mli", "k16", "k1"),
    **small("uint16", "pu", "mu16", "lowu", "highu", "piu", "ppu", "qpu", "wu", "wz", "lu", "k1u", "k2u", "sgu", "qsu"),
    **small("uint16", *["%s%d" % (n, r) for n in ("am", "aa", "mo", "ao") for r in range(3)]),
    **small("float32", "coff", "c640", "chalf", "nf", "nfk", "wf", "wg", "gg", "df", "t1", "t2", "t3", "t4", "t5"),
    **wide("md", "lg", "aw", "f320", "ssb", "sc0", "sc1", "sc2", "mw", "sm", "smh", "sw", "sgw", "qs"),
    **double("wa", "wb", "d1", "d2", "d3"), **{n: ("sbuf", [128, HALF + C], "float32") for n in ("qq", "qr", "cm")},
    "lw": ("sbuf", [128, 3 * C], "float32"), "tab": ("sbuf", [128, NCELL], "bfloat16"), "rs": ("sbuf", [128, 3 * C], "float32"),
    "pa": ("psum", [128, 2048], "float32"), "pb": ("psum", [128, 2048], "float32"),
}

SEMAPHORES = ["qV", "qS", "qT", "qG", "sent", "stored"] + ["ld_" + n for n in ("x", "u", "v", "wc", "ws", "pl", "ml", "qw", "mw")]
for _r in range(3):
    SEMAPHORES += ["arX%d" % _r, "arA%d" % _r, "arM%d" % _r]


def make_queues(g, T):
    queues = {"V": g.vector, "S": g.scalar, "T": g.tensor, "G": g, "Y": g.sync}
    count = {"V": 0, "S": 0, "T": 0, "G": 0}
    clocks = {}
    known = {q: {} for q in queues}
    writer, readers = {}, {}

    def merge(a, b):
        for k, n in b.items():
            if a.get(k, 0) < n:
                a[k] = n

    def need(q, sem, n):
        if known[q].get(sem, 0) >= n:
            return
        queues[q].wait_ge(T.sem[sem], n)
        if (sem, n) in clocks:
            merge(known[q], clocks[(sem, n)])
        known[q][sem] = n

    def waits(q, reads, writes):
        own = "q" + q
        want = {}
        for k in reads:
            if k in writer:
                s, n = writer[k]
                want[s] = max(want.get(s, 0), n)
        for k in writes:
            if k in writer:
                s, n = writer[k]
                want[s] = max(want.get(s, 0), n)
            for s, n in readers.get(k, {}).items():
                if s != own:
                    want[s] = max(want.get(s, 0), n)
        for s, n in want.items():
            need(q, s, n)

    def note(sem, n, reads, writes):
        for k in reads:
            r = readers.setdefault(k, {})
            r[sem] = max(r.get(sem, 0), n)
        for k in writes:
            writer[k] = (sem, n)
            readers[k] = {}

    def op(q, fn, reads, writes):
        waits(q, reads, writes)
        inst = fn(queues[q])
        count[q] += 1
        sem = "q" + q
        inst.then_inc(T.sem[sem], 1)
        c = dict(known[q])
        merge(c, clocks.get((sem, count[q] - 1), {}))
        c[sem] = count[q]
        clocks[(sem, count[q])] = c
        note(sem, count[q], reads, writes)

    def dma(q, pairs, sem, total, reads, writes):
        waits(q, reads, writes)
        for out, in_ in pairs:
            queues[q].dma_start(out, in_).then_inc(T.sem[sem], 16)
        note(sem, total, reads, writes)

    def arrives(sem, total, writes):
        note(sem, total, [], writes)

    return op, dma, arrives, waits, need, count


def rank_program(g, core, T, topo):
    rank = T.rank_of(core)
    if rank is None:
        return
    op, dma, arrives, waits, need, count = make_queues(g, T)
    sent = [0]

    def send(dst, out, in_, sem, key):
        waits("G", [key], [])
        rid, pid, _ = topo.addr(dst)
        g.remote_dma(out, in_, T.sem[sem], T.sem.sent, pid, rid, topo.mask(core, dst))
        sent[0] += len(topo.engines(core, dst))

    def copy(q, out, in_, reads, writes, scale=None):
        if q == "S":
            if scale is None:
                op("S", lambda e: e.activation(out, in_, AF.Copy), reads, writes)
            else:
                op("S", lambda e: e.activation(out, in_, AF.Copy, 0.0, scale), reads, writes)
        else:
            op("V", lambda e: e.tensor_copy(out, in_), reads, writes)

    def tt(out, a, b, o, reads, writes):
        op("V", lambda e: e.tensor_tensor(out, a, b, o), reads, writes)

    def ts(out, a, s1, o1, reads, writes, s2=None, o2=None):
        if o2 is None:
            op("V", lambda e: e.tensor_scalar(out, a, s1, None, o1), reads, writes)
        else:
            op("V", lambda e: e.tensor_scalar(out, a, s1, s2, o1, o2), reads, writes)

    def fill(ap, value, key):
        op("V", lambda e: e.memset(ap, value), [], [key])

    def ind(win, off, a=0, b=C):
        return T[win][:, a:b].indirect(T[off][:, 0:K])

    def scan(dst, src):
        op("V", lambda e: e.tensor_tensor_scan(T[dst][:], T.md[:], T[src][:, 0:C], 0.0, OP.add, OP.max), ["md", src], [dst])

    def ends(sc):
        return T[sc][:, 15:C:16]

    def take(out, sc, extra=None, o=None):
        ts(T[out][:], ends(sc), T.qoff[:, 0:1], OP.subtract, [sc, "qoff"], [out], extra, o)

    def mm(bank, lc, ls, rc, rs, reads, a):
        buf, b = bank
        op("T", lambda e: e.matmul_mx(T[buf][:, 512 * b:512 * b + C], T[lc][:, a:a + 128], T[ls][:, a:a + 128], T[rc][:], T[rs][:], True, True), reads, [(buf, b)])

    def quant(c, s, t, keys=None):
        op("V", lambda e: e.quantize_mx(T[c][:], T[s][:], T[t][:]), keys or [t], [c, s])

    def unit(b):
        op("V", lambda e: e.quantize_mx(T.ec[:, 128 * b:128 * b + 128], T.es[:, 128 * b:128 * b + 128], T.ebase[:, 3 - b:515 - b]), ["ebase"], [("ec", b)])

    dma("S", [(T.ut[:], T.u[:])], "ld_u", 16, [], ["ut"])
    dma("S", [(T.x0[:], T.x[:])], "ld_x", 16, [], ["x0"])
    dma("S", [(T.pli[:], T.pl[:])], "ld_pl", 16, [], ["pli"])
    dma("S", [(T.mli[:], T.ml[:])], "ld_ml", 16, [], ["mli"])
    dma("Y", [(T.qpi[i:128:16, :], T.ql[:]) for i in range(16)], "ld_qw", 256, [], ["qpi"])
    need("Y", "ld_x", 16)
    dma("Y", [(T.lc[:].bitcast(dt.uint8), T.wc[:])], "ld_wc", 16, [], ["lc"])
    dma("Y", [(T.ls[:], T.ws[:])], "ld_ws", 16, [], ["ls"])
    dma("Y", [(T.mpi[i:128:16, :], T.ml[:]) for i in range(16)], "ld_mw", 256, [], ["mpi"])
    dma("Y", [(T.vt[:], T.v[:])], "ld_v", 16, [], ["vt"])
    for r in range(3):
        e = len(topo.engines(T.cores[rank ^ STEP[r]], core))
        arrives("arX%d" % r, 2 * e, ["ac%d" % r, "as%d" % r])
        arrives("arA%d" % r, e, ["aa%d" % r])
        arrives("arM%d" % r, e, ["am%d" % r])

    def iota(name, a, b, step, base, mult, flag=False):
        op("G", lambda e: e.iota(T[name][:, a:b], [[step, b - a]], base, mult, allow_small_or_imprecise_dtypes=True) if flag else e.iota(T[name][:, a:b], [[step, b - a]], base, mult), [], [name])
    iota("pi1", 0, 1, 1, 0, 1)
    iota("ji", 0, C, 1, 4096, -1)
    iota("u8i", 0, 8, 16, 0, 0)
    iota("k1", 0, K, 1, 0, 0)
    iota("k16", 0, K, 16, 0, 0)
    fill(T.eone[:], 1.0, "eone")
    op("G", lambda e: e.affine_select(T.ebase[:], T.eone[:], [[-1, 516]], OP.is_equal, 0.0, 3, 4), ["eone"], ["ebase"])
    iota("wa", C, 2 * C, 1, C, 0, True)
    iota("wb", C, 2 * C, 1, C, 0, True)
    iota("cb", 0, C, 1, -160, 0, True)
    iota("cm", 0, C, 1, 0, 0, True)
    ts(T.pa1[:], T.pi1[:], 15, OP.bitwise_and, ["pi1"], ["pa1"])
    fill(T.d1[:, C:2 * C], 0.0, "d1")
    ts(T.pf1[:], T.pa1[:], 1.0, OP.mult, ["pa1"], ["pf1"])
    ts(T.ja[:], T.ji[:], 15, OP.bitwise_and, ["ji"], ["ja"])
    ts(T.p20[:], T.pf1[:], 20.0, OP.mult, ["pf1"], ["p20"])
    ts(T.qoff[:], T.pf1[:], -BIG, OP.mult, ["pf1"], ["qoff"], 15 * BIG, OP.add)
    ts(T.nqo[:], T.pf1[:], BIG, OP.mult, ["pf1"], ["nqo"], -15 * BIG, OP.add)
    ts(T.sc2[:], T.ja[:], 0.0, OP.is_equal, ["ja"], ["sc2"], -33 * BIG, OP.mult)
    copy("V", T.upick[:], T.u8i[:], ["u8i"], ["upick"])
    ts(T.piu[:], T.k1[:], T.p20[:, 0:1], OP.add, ["k1", "p20"], ["piu"])
    ts(T.coff[:], T.k16[:], T.pf1[:, 0:1], OP.add, ["k16", "pf1"], ["coff"])
    ts(T.md[:], T.sc2[:], BIG, OP.add, ["sc2"], ["md"])
    ts(T.nwg[:], T.nqo[:], float(SLOPE), OP.mult, ["nqo"], ["nwg"], float(SHIFT), OP.add)
    ts(T.c640[:], T.coff[:], float(2 * C), OP.add, ["coff"], ["c640"])
    ts(T.chalf[:], T.coff[:], 1.0 / HALF, OP.mult, ["coff"], ["chalf"])
    ts(T.nqh[:], T.nqo[:], float(HALF), OP.mult, ["nqo"], ["nqh"])
    ts(T.k16[:], T.pli[:], 15, OP.bitwise_and, ["pli"], ["k16"])
    ts(T.k1[:], T.pli[:], 4, OP.arith_shift_right, ["pli"], ["k1"])
    copy("V", T.pu[:], T.pli[:], ["pli"], ["pu"])
    ts(T.t1[:], T.k16[:], 20.0, OP.mult, ["k16"], ["t1"])
    fill(T.lw[:, 0:C], float(2 * UNMET), "lw")
    for n in ("d2", "d3"):
        copy("S", T[n][:, C:2 * C], T.d1[:, C:2 * C], ["d1"], [n])

    tt(T.t2[:], T.t1[:], T.k1[:], OP.add, ["t1", "k1"], ["t2"])
    quant("uc", "us", "ut")
    copy("V", T.ppu[:], T.t2[:], ["t2"], ["ppu"])
    op("S", lambda e: e.activation(T.urs[:], T.us[:].indirect(T.upick[:, 0:8]), AF.Copy), ["us", "upick"], ["urs"])
    op("V", lambda e: e.tensor_copy(T.urc[:].bitcast(dt.uint32), T.uc[:].bitcast(dt.uint32).indirect(T.upick[:, 0:8])), ["uc", "upick"], ["urc"])
    copy("V", T.gg[:], T.mli[:], ["mli"], ["gg"])
    copy("V", T.mu16[:], T.mli[:], ["mli"], ["mu16"])
    tt(T.wf[:], T.gg[:], T.coff[:], OP.min, ["gg", "coff"], ["wf"])
    tt(T.wg[:], T.gg[:], T.coff[:], OP.max, ["gg", "coff"], ["wg"])
    quant("tc0", "ts0", "x0")
    copy("V", T.lowu[:], T.wf[:], ["wf"], ["lowu"])
    copy("V", T.highu[:], T.wg[:], ["wg"], ["highu"])
    copy("S", T.aw[:], ind("qpi", "ppu"), ["qpi", "ppu"], ["aw"])
    copy("S", T.qq[:, 0:C], ind("qpi", "piu"), ["qpi", "piu"], ["qq"])
    unit(0)
    scan("sc0", "aw")

    qcur, qnew = "qq", "qr"
    for r in range(3):
        partner = T.cores[rank ^ STEP[r]]
        tc, tsn, zc, zs = "tc%d" % r, "ts%d" % r, "zc%d" % r, "zs%d" % r
        ao, mo, aa, am, ac, asn = "ao%d" % r, "mo%d" % r, "aa%d" % r, "am%d" % r, "ac%d" % r, "as%d" % r
        send(partner, T[ac][:].bitcast(dt.uint8), T[tc][:].bitcast(dt.uint8), "arX%d" % r, tc)
        send(partner, T[asn][:], T[tsn][:], "arX%d" % r, tsn)
        mm(("pb", 0), "urc", "urs", tc, tsn, ["urc", "urs", tc, tsn], 0)
        ts(T.f320[:], T.pb[:, 0:C], 0.0, OP.is_lt, [], ["f320", ("pb", 0)], float(C), OP.mult)
        copy("S", T.ssb[:], T.pb[:, 0:C], [], ["ssb", ("pb", 0)])
        take(ao, "sc0")
        if r == 0:
            unit(1)
        send(partner, T[aa][:], T[ao][:], "arA%d" % r, ao)
        tt(T.wa[:, 0:C], ind("f320", ao), T.aw[:], OP.add, ["f320", ao, "aw"], ["wa"])
        scan("sc0", "wa")
        take("wu", "sc0")
        if r == 0:
            unit(2)
            unit(3)
        for b in range(4):
            mm(("pa", b), "ec", "es", tc, tsn, [("ec", b), tc, tsn], 128 * b)
        for b in range(4):
            mm(("pb", b), "ec", "es", ac, asn, [("ec", b), ac, asn], 128 * b)

        def half(b):
            copy("S", T.fh[:, C * b:C * b + C], T.pb[:, 512 * b:512 * b + C], [], [("fh", b), ("pb", b)], 0.5)

        def ahead(b):
            copy("S", T.fa[:, C * b:C * b + C], ind("fh", aa, C * b, C * b + C), [("fh", b), aa], [("fa", b)])

        copy("S", T.wb[:, 0:C], ind("wa", "wu", 0, 2 * C), ["wa", "wu"], ["wb"])
        ts(T.d1[:, 0:C], T.wa[:, 0:C], float(C), OP.is_lt, ["wa"], ["d1"], 1.0, OP.add)
        scan("sc1", "f320")
        ts(T.d2[:, 0:C], ind("d1", "wu", 0, 2 * C), 1.0, OP.add, ["d1", "wu"], ["d2"])
        copy("S", T.wa[:, 0:C], ind("wb", "wu", 0, 2 * C), ["wb", "wu"], ["wa"])
        scan("sc0", "wa")
        take("wz", "sc0")
        copy("S", T.smh[:], T.d2[:, 0:C], ["d2"], ["smh"])
        ts(T.nf[:], ends("sc1"), T.qoff[:, 0:1], OP.subtract, ["sc1", "qoff"], ["nf"], 0.0, OP.is_equal)
        src, oth, dcur, d_a, d_b = "wa", "wb", "d2", "d3", "d1"
        lst, nxt = "wz", "wu"
        for i, k in enumerate(STAGES[1:], 1):
            copy("S", T[oth][:, 0:C], ind(src, lst, 0, 2 * C), [src, lst], [oth])
            tt(T[d_a][:, 0:C], ind(dcur, lst, 0, 2 * C), T.smh[:], OP.add, [dcur, lst, "smh"], [d_a])
            if i == 1:
                tt(T.t4[:], T.nf[:], T.c640[:], OP.mult, ["nf", "c640"], ["t4"])
            if k == 3:
                copy("S", T[src][:, 0:C], ind(oth, lst, 0, 2 * C), [oth, lst], [src])
                tt(T[d_b][:, 0:C], ind(d_a, lst, 0, 2 * C), T.smh[:], OP.add, [d_a, lst, "smh"], [d_b])
                copy("S", T.smh[:], T[d_b][:, 0:C], [d_b], ["smh"])
                scan("sc0", src)
                if i == 1:
                    ts(T.nfk[:], T.t4[:], T.qoff[:, 0:1], OP.add, ["t4", "qoff"], ["nfk"])
                take(nxt, "sc0")
                lst, nxt = nxt, lst
                dcur, d_b = d_b, dcur
            else:
                src, dcur = oth, d_a
        half(0)
        half(1)
        scan("sc0", src)
        scan("sc1", dcur)
        tt(T.t1[:], ends("sc0"), T.nfk[:], OP.max, ["sc0", "nfk"], ["t1"])
        op("S", lambda e: e.activation(T.wf[:], ends("sc0"), AF.Identity, T.nqo[:, 0:1]), ["sc0", "nqo"], ["wf"])
        op("S", lambda e: e.activation(T.wg[:], ends("sc0"), AF.Identity, T.nwg[:, 0:1], float(SLOPE)), ["sc0", "nwg"], ["wg"])
        take("wu", "sc0")
        ts(T.lu[:], T.t1[:], T.qoff[:, 0:1], OP.subtract, ["t1", "qoff"], ["lu"])
        take("df", "sc1")
        op("V", lambda e: e.tensor_copy(T.lw[:].indirect(T.lu[:, 0:K]), T[dcur][:, 0:C]), ["lu", dcur], ["lw"])
        half(2)
        half(3)
        copy("S", T.lg[:], ind("lw", "wu", 0, 2 * C), ["lw", "wu"], ["lg"])
        tt(T.t2[:], T.df[:], T.nf[:], OP.mult, ["df", "nf"], ["t2"])
        tt(T.gg[:], T.wf[:], T.wg[:], OP.max, ["wf", "wg"], ["gg"])
        tt(T.t3[:], T.gg[:], T.t2[:], OP.add, ["gg", "t2"], ["t3"])
        tt(T.t5[:], T.gg[:], ends("sc1"), OP.subtract, ["gg", "sc1"], ["t5"])
        copy("V", T.k1u[:], T.t3[:], ["t3"], ["k1u"])
        op("V", lambda e: e.tensor_copy(T.tab[:].indirect(T.k1u[:, 0:K]), T.cb[:]), ["k1u", "cb"], ["tab"])
        scan("sc2", "lg")
        tt(T.t4[:], ends("sc2"), T.t5[:], OP.add, ["sc2", "t5"], ["t4"])
        copy("V", T.k2u[:], T.t4[:], ["t4"], ["k2u"])
        ts(T.mw[:], T.tab[:].indirect(T.k2u[:, 0:K]), 160.0, OP.add, ["tab", "k2u"], ["mw"])
        for b in range(4):
            ahead(b)
        scan("sc0", "mw")
        take(mo, "sc0")
        send(partner, T[am][:], T[mo][:], "arM%d" % r, mo)
        copy("V", T.sm[:], ind("ssb", mo), ["ssb", mo], ["sm"])
        for b in (3, 2):
            copy("S", T.fo[:, C * b:C * b + C], T.pa[:, 512 * b:512 * b + C], [], [("fo", b), ("pa", b)], 32.0)

        def own(b):
            copy("S", T.fm[:, C * (b - 2):C * (b - 1)], ind("fo", mo, C * b, C * b + C), [("fo", b), mo], [("fm", b)])

        def early(b):
            c = C * (b - 2)
            tt(T.y3[:, c:c + C], T.pa[:, 512 * b:512 * b + C], T.fm[:, c:c + C], OP.add, [("fm", b)], [("y3", b), ("pa", b)])

        def turn(b):
            copy("S", T.xn[:, b:4 * C:4], ind("y3", mo, C * (b - 2), C * (b - 1)), [("y3", b), mo], [("xn", b)], 0.03125)

        def scaled(b):
            copy("S", T.rs[:, C * b:C * b + C], T.pa[:, 512 * b:512 * b + C], [], [("rs", b), ("pa", b)], 0.03125)

        def late(b):
            tt(T.xn[:, b:4 * C:4], ind("rs", mo, C * b, C * b + C), T.fo[:, C * b:C * b + C], OP.add, [("rs", b), mo, ("fo", b)], [("xn", b)])

        copy("S", T.smh[:], ind("sm", "highu"), ["sm", "highu"], ["smh"])
        if r == 0:
            copy("V", T.cm[:, HALF:HALF + C], ind("mpi", "piu"), ["mpi", "piu"], ["cm"])
            copy("S", T.qq[:, HALF:HALF + C], ind("qq", "mu16"), ["qq", "mu16"], [("qq", 1)])
        if r == 2:
            quant("vc", "vs", "vt")
        tt(T.sw[:], ind("sm", "lowu"), T.smh[:], OP.is_gt, ["sm", "lowu", "smh"], ["sw"])
        own(3)
        scan("sc1", "sw")

        def sigma():
            tt(T.t2[:], ends("sc1"), T.chalf[:], OP.add, ["sc1", "chalf"], ["t2"])
            ts(T.sgu[:], T.t2[:], float(HALF), OP.mult, ["t2", "nqh"], ["sgu"], T.nqh[:, 0:1], OP.add)

        def through():
            copy("S", T.qs[:], ind(qcur, "sgu", 0, HALF + C), [qcur, (qcur, 1), "sgu"], ["qs"])
            copy("S", T.sgw[:], ind("cm", "sgu", 0, HALF + C), ["cm", "sgu"], ["sgw"])

        if r < 2:
            sigma()
            through()
            copy("S", T.lg[:], ind("qs", "pu"), ["qs", "pu"], ["lg"])
        for b in range(4):
            tt(T.zt[:, b:4 * C:4], ind("fh", am, C * b, C * b + C), T.fa[:, C * b:C * b + C], OP.add, [("fh", b), ("fa", b), am], [("zt", b)])
        own(2)
        for b in range(2):
            copy("S", T.fo[:, C * b:C * b + C], T.pa[:, 512 * b:512 * b + C], [], [("fo", b), ("pa", b)])
        quant(zc, zs, "zt", [("zt", b) for b in range(4)])
        for b in (0, 2, 1, 3):
            mm(("pa", b), "lc", "ls", zc, zs, ["lc", "ls", zc, zs], 128 * b)
        if r < 2:
            scan("sc2", "lg")
            take("qpu", "sc2")
        else:
            sigma()
        scaled(0)
        early(2)
        late(0)
        scaled(1)
        turn(2)
        early(3)
        late(1)
        turn(3)
        if r < 2:
            copy("S", T.aw[:], ind("sgw", "qpu"), ["sgw", "qpu"], ["aw"])
        else:
            through()
        quant("tc%d" % (r + 1), "ts%d" % (r + 1), "xn", [("xn", b) for b in range(4)])
        if r < 2:
            scan("sc1", "qs")
            scan("sc0", "aw")
        else:
            scan("sc1", "qs")
        take("qsu", "sc1")
        copy("S", T[qnew][:, 0:C], ind("sgw", "qsu"), ["sgw", "qsu"], [qnew])
        if r < 2:
            copy("S", T[qnew][:, HALF:HALF + C], ind(qnew, "mu16"), [qnew, "mu16"], [(qnew, 1)])
        else:
            dma("S", [(T.qo[:], T[qnew][0:128:16, 0:C])], "stored", 16, [qnew], [])
        qcur, qnew = qnew, qcur
    dma("Y", [(T.oc[:], T.tc3[:].bitcast(dt.uint8))] + [(T.osc[4 * k:4 * k + 4, :], T.ts3[32 * k:32 * k + 4, :]) for k in range(4)], "stored", 96, ["tc3", "ts3"], [])
    mm(("pb", 0), "vc", "vs", "tc3", "ts3", ["vc", "vs", "tc3", "ts3"], 0)
    copy("V", T.sc2[:], T.pb[:, 0:C], [], ["sc2", ("pb", 0)])
    dma("Y", [(T.y[:], T.sc2[:])], "stored", 112, ["sc2"], [])
    g.sync.wait_ge(T.sem.stored, 112)
    g.wait_ge(T.sem.sent, sent[0])
    for q in ("V", "S", "T", "G"):
        need("G", "q" + q, count[q])
    for n, t in (("x", 16), ("u", 16), ("v", 16), ("wc", 16), ("ws", 16), ("pl", 16), ("ml", 16), ("qw", 256), ("mw", 256)):
        need("G", "ld_" + n, t)
